import numpy as np, ml_dtypes
CORES = [8,136,40,168]
N = 4
BF = ml_dtypes.bfloat16
def gentries(a):
    return np.ascontiguousarray(a.reshape(8, 16, -1).transpose(0, 2, 1)).reshape(8, -1)
def gtable(e):
    e = np.asarray(e); return np.ascontiguousarray(e.reshape(8, -1, 16).transpose(0, 2, 1)).reshape(128, -1).astype(np.int32)
def f(rng, *shape):
    return (rng.standard_normal(shape, dtype=np.float32) * np.exp2(rng.integers(-2, 3, shape[:-1] + (1,)))).astype(BF)
def wide(rng, *shape):
    v = f(rng, *shape).astype(np.float32); k = shape[:-2] + (1, shape[-1])
    return (v * np.exp2(rng.integers(-6, 7, k)) * (rng.random(k) > 0.0625)).astype(BF)
M, S, D, Q = 2048, 64, 8, 2
P = N // Q
def forest(rng, L, aside, bushy, zero=False):
    free = S + rng.permutation(M - S); n = S * (D - 1)
    chain = np.concatenate([np.arange(S)[:, None], free[:n].reshape(S, D - 1)], 1)
    p = np.arange(M); dep = np.full(M, -1); dep[chain] = np.arange(D); p[chain[:, 1:]] = chain[:, :-1]; rest = free[n:]
    if bushy:
        h = len(rest) // 2; p[rest[:h]] = rng.integers(0, S); p[rest[h:]] = chain[rng.integers(0, S), D - 2]
    else:
        lev = rng.integers(1, D, len(rest))
        for d in range(1, D):
            v = rest[lev == d]; p[v] = rng.choice(np.flatnonzero(dep == d - 1), len(v)); dep[v] = d
    kids = S + rng.permutation(M - S); o = kids[np.argsort(p[kids], kind="stable")]; q = p[o]
    sib = np.zeros(M, np.int64); sib[o] = np.arange(M - S) - np.searchsorted(q, q); c = np.bincount(q, minlength=M)
    base = rng.integers(0, 4096, M); step = 2 * rng.integers(0, 2048, M) + 1
    if zero: base[0] = 0
    x = np.where((c > 0) & (rng.random(M) < 0.7), (rng.random(M) * c).astype(np.int64), c + (rng.random(M) * (4096 - c)).astype(np.int64))
    x[chain[:, :-1]] = sib[chain[:, 1:]]
    e = np.flatnonzero(L < D - 1); b = chain[e, L[e]]; w = sib[chain[e, L[e] + 1]]; cb = c[b]
    other = (w + 1 + (rng.random(len(e)) * (cb - 1)).astype(np.int64)) % cb; none = cb + (rng.random(len(e)) * (4096 - cb)).astype(np.int64)
    x[b] = np.where((cb > 1) & (rng.random(len(e)) < aside), other, none)
    t = (base + step * x) % 4096
    k = np.zeros(M, np.int64); k[o] = (base[q] + step[q] * sib[o]) % 4096
    k[:S] = np.where(rng.random(S) < 0.5, t[:S], rng.integers(0, 4096, S))
    return p, k, t
def shards(rng, t, sc, tie):
    v = sc * 4096 + t; win = rng.integers(0, N, t.shape); u = rng.random((N,) + t.shape)
    o = np.where(rng.random(t.shape) < tie, sc * 4096 + (u * (t + 1)).astype(np.int64), (u * (v + 1)).astype(np.int64))
    o = np.where((np.arange(N)[:, None, None, None] == win) | (rng.random(o.shape) < 0.03125), v, np.minimum(o, v))
    return np.ascontiguousarray(o.transpose(0, 2, 1, 3)).reshape(N, 8, N * M).astype(np.int32)
def draw(rng, L, aside=0.5, bushy=False, tie=0.125, uneven=False, zero=False):
    a = [[forest(rng, L[q, g], aside, bushy, zero) for g in range(8)] for q in range(N)]
    p, k, t = [np.array([[a[q][g][i] for g in range(8)] for q in range(N)]) for i in range(3)]
    sc = rng.integers(0, 4096, t.shape)
    if uneven: sc = 4095 >> rng.integers(0, 13, t.shape)
    return {"par": np.stack([gtable(p[q]) for q in range(N)]), "tok": k.astype(np.int32), "best": shards(rng, t, sc, tie), "kv": f(rng, N, 128, Q * M)}
def setup_inputs(rng):
    return draw(rng, rng.integers(0, D, (N, 8, S)))
def setup_inputs_full(rng):
    return draw(rng, np.full((N, 8, S), D - 1))
def setup_inputs_cut(rng):
    return draw(rng, rng.choice(np.array([0, 1, D - 2]), (N, 8, S)), aside=0.0, zero=True)
def setup_inputs_ties(rng):
    return draw(rng, rng.integers(0, D, (N, 8, S)), tie=1.0)
def setup_inputs_bushy(rng):
    return draw(rng, rng.integers(0, D, (N, 8, S)), bushy=True)
def setup_inputs_spread(rng):
    d = draw(rng, rng.integers(0, D, (N, 8, S)), uneven=True); d["kv"] = wide(rng, N, 128, Q * M); return d
def check_inputs(d):
    bad = []; p = np.stack([gentries(a) for a in d["par"]]).astype(np.int64); k = d["tok"].astype(np.int64); b = d["best"]
    if not np.isfinite(d["kv"].astype(np.float32)).all(): bad.append("finite")
    if b.min() < 0 or b.max() >= 1 << 24: bad.append("best")
    if k.min() < 0 or k.max() > 4095: bad.append("tokens")
    if p.min() < 0 or p.max() >= M: return bad + ["parents"]
    if (p[:, :, :S] != np.arange(S)).any(): bad.append("roots")
    a = p
    for i in range(D - 2): a = np.take_along_axis(p, a, 2)
    if (a >= S).any(): bad.append("depth")
    w = np.sort((p * 4096 + k)[:, :, S:], axis=2)
    if (w[:, :, 1:] == w[:, :, :-1]).any(): bad.append("children")
    return bad
def reference(par, tok, best, kv):
    p = np.stack([gentries(a) for a in par]).astype(np.int64)
    t = np.max(best, axis=0).reshape(8, N, M).transpose(1, 0, 2) & 4095
    ok = (np.arange(M) < S) | (tok == np.take_along_axis(t, p, 2))
    a = np.broadcast_to(np.arange(M), p.shape); acc = np.ones(p.shape, bool); dep = np.zeros(p.shape, np.int64)
    for i in range(D):
        acc = acc & np.take_along_axis(ok, a, 2); dep = dep + (a >= S); a = np.take_along_axis(p, a, 2)
    y = np.zeros((N, 128, Q * S * D), BF)
    for r in range(N):
        out = y[r].reshape(8, 16, Q * S * D)
        for i in range(Q):
            q = P * i + r % P; k = kv[r][:, i * M:(i + 1) * M].reshape(8, 16, M)
            g, j = np.nonzero(acc[q])
            out[g, :, (i * S + a[q, g, j]) * D + dep[q, g, j]] = k[g, :, j]
    return {"y": y}

@@ -1,0 +1,340 @@
+from concourse.mybir import AluOpType as Op, ActivationFunctionType as Fn
+
+CH = [(4, 42), (42, 94), (94, 128)]
+VS = 56
+NODE, REG = 2048, 2064
+MID = NODE + REG
+ZC = 258
+NZ = REG // ZC
+Z0 = 4
+ZR = (0, 0, 1, 3, 6)
+ZA = MID + NODE + ZR[4] * ZC
+ZB = 2 * MID - 128
+HV = 13
+SP = {1: slice(0, None, 2), 2: slice(1, None, 2), 3: slice(0, None)}
+W = 2.0 ** 24
+EARLY = 5
+KV1, KV2 = (1, 2), (6,)
+
+I32 = ("sbuf", [128, 128], "int32")
+U16 = ("sbuf", [128, 128], "uint16")
+B16 = ("sbuf", [128, 128], "bfloat16")
+F16 = ("sbuf", [128, 128], "float16")
+PS = ("psum", [128, 512], "float32")
+
+
+def sb(k, d="float32"):
+    return ("sbuf", [128, k], d)
+
+
+SCRATCH = {
+    "own": I32, "snd": sb(384, "int32"), "land1": I32, "land2": I32, "land3": I32, "mx": I32, "tgt": I32,
+    "tokc": I32, "tokf": F16, "part": I32, "parlo": I32, "parhi": I32, "lo": U16, "hif": B16, "pcol": sb(128),
+    "sm": sb(32, "int32"), "d15": sb(32, "int32"), "pmod": sb(1), "pb": sb(1), "qc": sb(1), "mb": B16, "ab": B16, "grp": B16,
+    "mcol": sb(16, "bfloat16"), "msk": sb(32), "mr": B16, "mrf": F16, "hx": sb(2048, "bfloat16"),
+    "sel": sb(2048, "float16"), "wi": sb(144, "bfloat16"), "tab": sb(144, "float16"), "cst": B16,
+    "c16r": B16, "cc": sb(64), "c1": sb(32), "c2": sb(32), "sc": sb(1), "jrow": sb(1984),
+    "tokx": sb(2048), "eq": sb(2048, "float16"), "offi": sb(128), "off": U16, "zero": sb(ZC), "ww": sb(2 * MID),
+    "vs": sb(896), "ts": sb(896), "ls": sb(32, "uint16"), "k2": sb(32, "uint16"),
+    "kva": sb(2080, "bfloat16"), "kvb": sb(2080, "bfloat16"), "ya": sb(512, "bfloat16"), "yb": sb(512, "bfloat16"),
+    "tr0": PS, "tr1": PS, "tr2": PS, "tr3": PS, "ps0": PS, "ps1": PS, "ps2": PS, "pm": PS,
+}
+SEMAPHORES = (["ld1", "ld2", "ld3", "ldown", "ldtok", "ldpar", "ldkv", "sent", "arr1", "arr2", "arr3", "lst", "lst2", "lsent",
+               "st1", "gsm", "gmb", "gmr", "gwi", "gpre", "vc1", "vcc", "vsc",
+               "vz", "vzb", "vkz", "vcst", "vsel", "vmr", "vtok", "vpar", "vpcol", "vhi", "vhf", "vhx", "ahx", "vlist", "vpmod",
+               "vpb", "vqc", "vtab", "vd15", "vmsk", "vmcol", "aab", "vgrp", "vm1", "vm2", "vm30", "vm31", "vtgt", "vyb", "aya",
+               "ayb", "afa", "afb", "ev0", "ev1", "ev2", "ev3", "ptr0", "ptr1", "ptr2", "ptr3", "sca", "scv"]
+              + ["%s%d%d" % (w, d, h) for w in ("x", "y", "t", "l") for d in range(7) for h in range(2)]
+              + ["%s%d" % (w, c) for w in ("veq", "pok", "vo", "voff", "gj") for c in range(len(CH))])
+
+
+def rank_program(g, core, T, topo):
+    r = T.rank_of(core)
+    if r is None:
+        return
+    S = T.sem
+    cores = T.cores
+    n = len(cores)
+    V, A, P, Y = g.vector, g.scalar, g.tensor, g.sync
+    mate = (r + 2) % n
+    mine, other = r // 2, 1 - r // 2
+    low = {"allow_small_or_imprecise_dtypes": True}
+    ps = [T.ps0, T.ps1, T.ps2]
+
+    def blk(q):
+        return T.best[:, q * 2048:(q + 1) * 2048]
+
+    Y.dma_start(T.snd[:, 0:128], blk((r + 1) % n)).then_inc(S.ld1, 16)
+    A.dma_start(T.part[:], T.par[:]).then_inc(S.ldpar, 16)
+    Y.dma_start(T.tokc[:], T.tok[:]).then_inc(S.ldtok, 16)
+    A.dma_start(T.snd[:, 128:256], blk((r + 2) % n)).then_inc(S.ld2, 16)
+    Y.dma_start(T.snd[:, 256:384], blk((r + 3) % n)).then_inc(S.ld3, 16)
+    A.dma_start(T.own[:], blk(r)).then_inc(S.ldown, 16)
+    eng = {k: topo.engines(core, cores[(r + k) % n])[SP[k]] for k in (1, 2, 3)}
+    ne = {k: len(eng[k]) for k in eng}
+    Y.wait_ge(S.vkz, 2)
+    Y.wait_ge(S.sent, sum(ne.values()))
+    Y.dma_start(T.kva[:, 17:2065], T.kv[:, mine * 2048:(mine + 1) * 2048]).then_inc(S.ldkv, 16)
+    Y.dma_start(T.kvb[:, 17:2065], T.kv[:, other * 2048:(other + 1) * 2048]).then_inc(S.ldkv, 16)
+
+    g.iota(T.mb[:], [[-16, 8], [0, 16]], 0, 1, **low).then_inc(S.gmb, 1)
+    g.iota(T.sm[:], [[-1, 32]], 0, 1).then_inc(S.gsm, 1)
+    g.iota(T.mr[:], [[0, 8], [-4096, 16]], 0, 0, **low).then_inc(S.gmr, 1)
+    for k in (1, 2, 3):
+        dst = cores[(r + k) % n]
+        rid, pid = topo.addr(dst, core)
+        g.wait_ge(S["ld%d" % k], 16)
+        g.remote_dma(T["land%d" % k][:], T.snd[:, (k - 1) * 128:k * 128], S["arr%d" % k], S.sent, pid, rid,
+                     sum(1 << e for e in eng[k]))
+    g.iota(T.wi[:], [[1, 144]], -15, -1, **low).then_inc(S.gwi, 1)
+    g.iota(T.c16r[:], [[16, 128]], 0, 0, **low).then_inc(S.gpre, 1)
+    for c, (c0, c1) in enumerate(CH):
+        g.iota(T.jrow[:, 16 * c0 - 64:16 * c1 - 64], [[1, 16 * (c1 - c0)]], 16 * c0 + 1, 0, **low).then_inc(S["gj%d" % c], 1)
+
+    V.memset(T.zero[:], 0.0).then_inc(S.vz, 1)
+    V.wait_ge(S.gmb, 1)
+    for a in range(16):
+        V.tensor_scalar(T.sel[:, 128 * a:128 * a + 128], T.mb[:], float(a), None, Op.is_equal).then_inc(S.vsel, 1)
+    V.wait_ge(S.gsm, 1)
+    V.tensor_scalar(T.d15[:], T.sm[:], 15, None, Op.bitwise_and).then_inc(S.vd15, 1)
+    V.wait_ge(S.gmr, 1)
+    V.tensor_copy(T.mrf[:], T.mr[:]).then_inc(S.vmr, 1)
+    V.wait_ge(S.aab, 1)
+    V.tensor_scalar(T.grp[:], T.ab[:], 8.0, 2048.0, Op.is_lt, Op.mult).then_inc(S.vgrp, 1)
+    V.wait_ge(S.vd15, 1)
+    V.tensor_scalar(T.msk[:], T.d15[:], 0.0, None, Op.is_equal).then_inc(S.vmsk, 1)
+    V.tensor_scalar(T.mcol[:], T.d15[:, 0:16], 0.0, None, Op.is_equal).then_inc(S.vmcol, 1)
+    V.tensor_copy(T.pmod[:], T.d15[:, 0:1]).then_inc(S.vpmod, 1)
+    V.memset(T.cst[:], 2.0 ** -19).then_inc(S.vcst, 1)
+    V.memset(T.cc[:, 1:64:2], 1.0).then_inc(S.vcc, 1)
+    V.memset(T.kva[:, 16:32], 0.0).then_inc(S.vkz, 1)
+    V.memset(T.kvb[:, 16:32], 0.0).then_inc(S.vkz, 1)
+    V.wait_ge(S.vpmod, 1)
+    V.tensor_scalar(T.pb[:], T.pmod[:], -4096.0, 2048.0, Op.mult, Op.add).then_inc(S.vpb, 1)
+    V.tensor_scalar(T.qc[:], T.pmod[:], -1.0 / 4096, (NODE + 1) / 4096, Op.mult, Op.add).then_inc(S.vqc, 1)
+    V.wait_ge(S.ldpar, 16)
+    V.tensor_scalar(T.parhi[:], T.part[:], 7, None, Op.arith_shift_right).then_inc(S.vhi, 1)
+    V.wait_ge(S.ldtok, 16)
+    V.tensor_scalar(T.tokf[:], T.tokc[:], -2048.0, None, Op.add).then_inc(S.vtok, 1)
+    V.wait_ge(S.vhi, 1)
+    V.tensor_scalar(T.hif[:], T.parhi[:], 2.0, None, Op.mult).then_inc(S.vhf, 1)
+    V.tensor_scalar(T.parlo[:], T.part[:], 127, None, Op.bitwise_and).then_inc(S.vpar, 1)
+    V.wait_ge(S.vmcol, 1)
+    V.wait_ge(S.vhf, 1)
+    for i in range(HV):
+        V.tensor_scalar(T.hx[:, i:2048:16], T.hif[:], T.mcol[:, i:i + 1], None, Op.mult).then_inc(S.vhx, 1)
+    V.memset(T.ww[:, ZA:ZB], 0.0).then_inc(S.vzb, 1)
+
+    def offs(b):
+        P.matmul(T["tr%d" % b][:, 0:512], T.mrf[:], T.sel[:, 0:512], True, False).then_inc(S["ptr%d" % b], 1)
+
+    def toks(b):
+        for k in range(4):
+            a = 4 * b + k
+            P.matmul(T["tr%d" % b][:, 128 * k:128 * k + 128], T.sel[:, 128 * a:128 * a + 128], T.tokf[:], False,
+                     b > 1 and k == 3).then_inc(S["ptr%d" % b], 1)
+
+    def places(b):
+        P.matmul(T["tr%d" % b][:, 0:512], T.grp[:], T.hx[:, 512 * b:512 * b + 512], b > 1, b < 2).then_inc(S["ptr%d" % b], 1)
+
+    P.wait_ge(S.vsel, 16)
+    P.wait_ge(S.vmr, 1)
+    offs(0)
+    offs(1)
+    P.wait_ge(S.vtok, 1)
+    toks(0)
+    toks(1)
+    P.wait_ge(S.vgrp, 1)
+    P.wait_ge(S.vhx, HV)
+    P.wait_ge(S.ahx, 16 - HV)
+    places(0)
+    places(1)
+    for b in (2, 3):
+        places(b)
+        toks(b)
+    P.wait_ge(S.vcst, 1)
+    P.wait_ge(S.gpre, 1)
+    for c, (c0, c1) in enumerate(CH):
+        P.matmul(ps[c][:, 0:c1 - c0], T.cst[:], T.c16r[:, c0:c1], True, False).then_inc(S["pok%d" % c], 1)
+    P.wait_ge(S.vtab, 1)
+
+    def zeros(b, k0, k1, sem):
+        for k in range(k0, k1):
+            A.activation(T.ww[:, b + ZC * k:b + ZC * k + ZC], T.zero[:], Fn.Silu).then_inc(sem, 1)
+
+    A.wait_ge(S.gmb, 1)
+    A.activation(T.ab[:], T.mb[:], Fn.Abs, bias=-7.5).then_inc(S.aab, 1)
+    A.wait_ge(S.vz, 1)
+    zeros(NODE, 0, Z0, S.afa)
+    A.wait_ge(S.vmsk, 1)
+    A.wait_ge(S.vhf, 1)
+    for i in range(HV, 16):
+        A.activation(T.hx[:, i:2048:16], T.hif[:], Fn.Copy, scale=T.msk[:, i:i + 1]).then_inc(S.ahx, 1)
+    zeros(NODE, Z0, NZ, S.afa)
+    A.wait_ge(S.vpb, 1)
+    for b in range(4):
+        A.wait_ge(S["ptr%d" % b], 6 if b < 2 else 5)
+        A.activation(T.tokx[:, 512 * b:512 * b + 512], T["tr%d" % b][:], Fn.Identity, bias=2048.0 if b < 2 else T.pb[:]).then_inc(
+            S["ev%d" % b], 1)
+        zeros(MID + NODE, ZR[b], ZR[b + 1], S.afb)
+
+    V.wait_ge(S.ldown, 16)
+    prev = T.own[:, 0:128]
+    for k in (1, 2):
+        m = T.pm[:, 128 * k - 128:128 * k]
+        V.wait_ge(S["arr%d" % k], ne[k])
+        V.tensor_tensor(m, prev, T["land%d" % k][:], Op.max).then_inc(S["vm%d" % k], 1)
+        if k == 1:
+            V.wait_ge(S.gwi, 1)
+            V.tensor_scalar(T.tab[:], T.wi[:], T.pmod[:], 0.0, Op.add, Op.is_equal).then_inc(S.vtab, 1)
+        else:
+            V.wait_ge(S.vpar, 1)
+            V.tensor_copy(T.lo[:], T.parlo[:]).then_inc(S.vlist, 1)
+        V.wait_ge(S["vm%d" % k], 1)
+        prev = m
+    V.wait_ge(S.arr3, ne[3])
+    for h in range(2):
+        V.tensor_tensor(T.mx[:, 64 * h:64 * h + 64], T.pm[:, 128 + 64 * h:192 + 64 * h], T.land3[:, 64 * h:64 * h + 64],
+                        Op.max).then_inc(S["vm3%d" % h], 1)
+    for h in range(2):
+        V.wait_ge(S["vm3%d" % h], 1)
+        V.tensor_scalar(T.tgt[:, 64 * h:64 * h + 64], T.mx[:, 64 * h:64 * h + 64], 4095, None, Op.bitwise_and).then_inc(S.vtgt, 1)
+    V.wait_ge(S.vqc, 1)
+    V.tensor_scalar(T.pcol[:], T.part[:], 1.0 / 4096, T.qc[:], Op.mult, Op.add).then_inc(S.vpcol, 1)
+    V.wait_ge(S.vlist, 1)
+    V.wait_ge(S.vtgt, 2)
+
+    def match(c):
+        c0, c1 = CH[c]
+        for b in range(4):
+            if c0 < 32 * b + 32 and c1 > 32 * b:
+                V.wait_ge(S["ev%d" % b], 1)
+        V.tensor_tensor(T.eq[:, 16 * c0:16 * c1], T.tgt[:, 0:128].indirect(T.lo[:, c0:c1]), T.tokx[:, 16 * c0:16 * c1],
+                        Op.is_equal).then_inc(S["veq%d" % c], 1)
+        P.wait_ge(S["veq%d" % c], 1)
+        for i in range(16):
+            P.matmul(ps[c][:, 0:c1 - c0], T.tab[:, 15 - i:143 - i], T.eq[:, 16 * c0 + i:16 * c1:16],
+                     False, i == 15).then_inc(S["pok%d" % c], 1)
+
+    def offsets(c):
+        c0, c1 = CH[c]
+        V.wait_ge(S.vpcol, 1)
+        V.wait_ge(S["pok%d" % c], 17)
+        V.tensor_tensor(T.offi[:, c0:c1], ps[c][:, 0:c1 - c0], T.pcol[:, c0:c1], Op.min).then_inc(S["vo%d" % c], 1)
+        if c == 0:
+            V.tensor_scalar(T.c1[:], T.d15[:], 15.0, W, Op.is_equal, Op.mult).then_inc(S.vc1, 1)
+            V.tensor_scalar(T.c2[:], T.d15[:], 1.0, None, Op.min).then_inc(S.vc1, 1)
+        elif c == 1:
+            V.memset(T.ww[:, ZB:2 * MID], 0.0).then_inc(S.vzb, 1)
+        else:
+            V.tensor_scalar(T.sc[:], T.pmod[:], 15.0, 1.0 / W, Op.is_equal, Op.max).then_inc(S.vsc, 1)
+            V.wait_ge(S.vc1, 2)
+            V.tensor_tensor(T.cc[:, 0:64:2], T.c1[:], T.c2[:], Op.max).then_inc(S.vcc, 1)
+        V.wait_ge(S["vo%d" % c], 1)
+        V.tensor_scalar(T.off[:, c0:c1], T.offi[:, c0:c1], 4096.0, T.pmod[:], Op.mult, Op.add).then_inc(S["voff%d" % c], 1)
+
+    match(0)
+    match(1)
+    offsets(0)
+    match(2)
+    offsets(1)
+    A.wait_ge(S.afa, NZ)
+    for k, c in enumerate((0, 2)):
+        c0, c1 = CH[c]
+        A.wait_ge(S["gj%d" % c], 1)
+        A.wait_ge(S["voff%d" % c], 1)
+        if k:
+            A.wait_ge(S.sca, 1)
+        A.activation(T.ww[:, 0:MID].indirect(T.off[:, c0:c1]), T.jrow[:, 16 * c0 - 64:16 * c1 - 64], Fn.Silu).then_inc(S.sca, 1)
+    V.wait_ge(S.vzb, 2)
+    V.wait_ge(S.afb, ZR[4])
+    V.wait_ge(S.gj1, 1)
+    V.wait_ge(S.voff1, 1)
+    for k, (c0, c1) in enumerate(((CH[1][0], VS), (VS, CH[1][1]))):
+        if k:
+            offsets(2)
+            V.wait_ge(S.scv, 1)
+        V.tensor_copy(T.ww[:, MID:2 * MID].indirect(T.off[:, c0:c1]), T.jrow[:, 16 * c0 - 64:16 * c1 - 64]).then_inc(S.scv, 1)
+
+    def look(q, d, w):
+        w0 = (NODE, MID + NODE)[w]
+        for h in range(2 if d else 1):
+            e0, b = 128 * d + 64 * h, 4 * d + 2 * h
+            if d:
+                q.wait_ge(S["l%d%d" % (d - 1, h)], 1)
+                src, out = T.ww[:, w0:w0 + REG].indirect(T.ls[:, b:b + 2]), T.vs[:, e0 + w:e0 + 64:2]
+            else:
+                src, out = T.ww[:, w0 + 1:w0 + 65], T.vs[:, w:128:2]
+            if w:
+                q.tensor_copy(out, src).then_inc(S["y%d%d" % (d, h)], 1)
+            else:
+                q.activation(out, src, Fn.Copy).then_inc(S["x%d%d" % (d, h)], 1)
+
+    V.wait_ge(S.scv, 2)
+    for d in range(7):
+        look(V, d, 1)
+        if d == 0:
+            V.wait_ge(S.vcc, 2)
+            V.wait_ge(S.vsc, 1)
+        for h in range(2):
+            e0 = 128 * d + 64 * h
+            for w in "yx":
+                V.wait_ge(S["%s%d%d" % (w, d, h if d else 0)], 1)
+            V.tensor_tensor_scan(T.ts[:, e0:e0 + 64], T.cc[:], T.vs[:, e0:e0 + 64], 0.0, Op.mult, Op.add).then_inc(
+                S["t%d%d" % (d, h)], 1)
+        for h in range(2):
+            e0, b = 128 * d + 64 * h, 4 * d + 4 + 2 * h
+            V.wait_ge(S["t%d%d" % (d, h)], 1)
+            V.tensor_scalar(T.ls[:, b:b + 2], T.ts[:, e0 + 31:e0 + 64:32], T.sc[:], 0.25, Op.mult, Op.add).then_inc(
+                S["l%d%d" % (d, h)], 1)
+
+    def list_of(q, d):
+        q.wait_ge(S["l%d0" % (d - 1)], 1)
+        q.wait_ge(S["l%d1" % (d - 1)], 1)
+
+    dst = cores[mate]
+    rid, pid = topo.addr(dst, core)
+    nl = len(topo.engines(core, dst))
+    m = 4 * EARLY + 4
+    for d in range(1, EARLY + 1):
+        list_of(g, d)
+    g.remote_dma(T.k2[:, 4:m], T.ls[:, 4:m], S.lst, S.lsent, pid, rid, topo.mask(core, dst))
+    for d in range(EARLY + 1, 8):
+        list_of(g, d)
+    g.remote_dma(T.k2[:, m:32], T.ls[:, m:32], S.lst2, S.lsent, pid, rid, topo.mask(core, dst))
+    g.wait_ge(S.lsent, 2 * nl)
+    ka, kb = T.kva[:, 16:2065], T.kvb[:, 16:2065]
+    A.wait_ge(S.sca, 2)
+    for d in range(8):
+        if d < 7:
+            look(A, d, 0)
+        else:
+            list_of(A, d)
+        if d == 0:
+            A.wait_ge(S.ldkv, 32)
+        A.activation(T.ya[:, d:512:8], ka.indirect(T.ls[:, 4 * d:4 * d + 4]) if d else T.kva[:, 17:81], Fn.Copy).then_inc(S.aya, 1)
+    Y.wait_ge(S.aya, 8)
+    Y.dma_start(T.y[:, 512 * mine:512 * mine + 512], T.ya[:]).then_inc(S.st1, 16)
+    V.wait_ge(S.ldkv, 32)
+    V.tensor_copy(T.yb[:, 0:512:8], T.kvb[:, 17:81]).then_inc(S.vyb, 1)
+
+    def keys(d, v):
+        out, src = T.yb[:, d:512:8], kb.indirect(T.k2[:, 4 * d:4 * d + 4])
+        if v:
+            V.tensor_copy(out, src).then_inc(S.vyb, 1)
+        else:
+            A.activation(out, src, Fn.Copy).then_inc(S.ayb, 1)
+
+    V.wait_ge(S.lst, nl)
+    A.wait_ge(S.lst, nl)
+    for d in range(1, EARLY + 1):
+        keys(d, d in KV1)
+    V.wait_ge(S.lst2, nl)
+    A.wait_ge(S.lst2, nl)
+    for d in range(EARLY + 1, 8):
+        keys(d, d in KV2)
+    nk = 1 + len(KV1) + len(KV2)
+    Y.wait_ge(S.vyb, nk)
+    Y.wait_ge(S.ayb, 8 - nk)
+    Y.dma_start(T.y[:, 512 * other:512 * other + 512], T.yb[:]).then_inc(S.st1, 16)
+    Y.wait_ge(S.st1, 32)

@@ -1,16 +1,18 @@
 from concourse.mybir import AluOpType as Op, ActivationFunctionType as Fn
 
-CH = [(4, 42), (42, 94), (94, 128)]
-VS = 56
-NODE, REG = 2048, 2064
-MID = NODE + REG
-ZC = 258
-NZ = REG // ZC
-Z0 = 4
-ZR = (0, 0, 1, 3, 6)
-ZA = MID + NODE + ZR[4] * ZC
-ZB = 2 * MID - 128
-HV = 13
+CH = [(4, 42), (42, 96), (96, 128)]
+MV = [(4, 42), (42, 52)]
+MS = [(52, 64), (64, 96), (96, 128)]
+SS = [(4, 42), (96, 128)]
+SV = [(42, 56), (56, 96)]
+ORDER = "v0 v1 c0 c1 o0 c2 o1 f0 s0 o2 s1"
+NODE, REG = 2048, 2049
+BIG = 2.0 ** 30
+ZC = 257
+NZ = 8
+ZR = (2, 2, 2, 3, 8)
+LS = 124
+HI = 144.0
 SP = {1: slice(0, None, 2), 2: slice(1, None, 2), 3: slice(0, None)}
 W = 2.0 ** 24
 EARLY = 5
@@ -28,24 +30,29 @@ def sb(k, d="float32"):
 
 
 SCRATCH = {
-    "own": I32, "snd": sb(384, "int32"), "land1": I32, "land2": I32, "land3": I32, "mx": I32, "tgt": I32,
-    "tokc": I32, "tokf": F16, "part": I32, "parlo": I32, "parhi": I32, "lo": U16, "hif": B16, "pcol": sb(128),
-    "sm": sb(32, "int32"), "d15": sb(32, "int32"), "pmod": sb(1), "pb": sb(1), "qc": sb(1), "mb": B16, "ab": B16, "grp": B16,
-    "mcol": sb(16, "bfloat16"), "msk": sb(32), "mr": B16, "mrf": F16, "hx": sb(2048, "bfloat16"),
-    "sel": sb(2048, "float16"), "wi": sb(144, "bfloat16"), "tab": sb(144, "float16"), "cst": B16,
-    "c16r": B16, "cc": sb(64), "c1": sb(32), "c2": sb(32), "sc": sb(1), "jrow": sb(1984),
-    "tokx": sb(2048), "eq": sb(2048, "float16"), "offi": sb(128), "off": U16, "zero": sb(ZC), "ww": sb(2 * MID),
-    "vs": sb(896), "ts": sb(896), "ls": sb(32, "uint16"), "k2": sb(32, "uint16"),
+    "own": I32, "snd": ("dram", [3, 128, 128], "int32"), "land1": I32, "land2": I32, "land3": I32, "mx": I32, "tgt": I32,
+    "tokc": I32, "tokf": F16, "part": I32, "parlo": I32, "lo": U16, "hif": B16, "pcol": sb(128),
+    "sm": sb(16, "int32"), "d15": sb(16, "int32"), "pmod": sb(1), "pb": sb(1), "nb": sb(1), "mb": B16, "ab": B16,
+    "grp": B16, "mcol": sb(16, "bfloat16"), "hx": sb(2048, "bfloat16"),
+    "sel": sb(2048, "float16"), "tab": sb(144, "float16"), "cst": B16, "mr": B16,
+    "c16r": B16, "cc": sb(32), "c1": sb(16), "c2": sb(16), "jrow": sb(2048),
+    "eq": sb(2048, "float16"), "off": U16, "zero": sb(ZC), "ww": sb(NODE + NZ * ZC), "wv": sb(NODE + REG),
+    "vs": sb(896), "ls": sb(LS + 32, "uint16"), "k2": sb(32, "uint16"),
     "kva": sb(2080, "bfloat16"), "kvb": sb(2080, "bfloat16"), "ya": sb(512, "bfloat16"), "yb": sb(512, "bfloat16"),
     "tr0": PS, "tr1": PS, "tr2": PS, "tr3": PS, "ps0": PS, "ps1": PS, "ps2": PS, "pm": PS,
 }
-SEMAPHORES = (["ld1", "ld2", "ld3", "ldown", "ldtok", "ldpar", "ldkv", "sent", "arr1", "arr2", "arr3", "lst", "lst2", "lsent",
-               "st1", "gsm", "gmb", "gmr", "gwi", "gpre", "vc1", "vcc", "vsc",
-               "vz", "vzb", "vkz", "vcst", "vsel", "vmr", "vtok", "vpar", "vpcol", "vhi", "vhf", "vhx", "ahx", "vlist", "vpmod",
-               "vpb", "vqc", "vtab", "vd15", "vmsk", "vmcol", "aab", "vgrp", "vm1", "vm2", "vm30", "vm31", "vtgt", "vyb", "aya",
-               "ayb", "afa", "afb", "ev0", "ev1", "ev2", "ev3", "ptr0", "ptr1", "ptr2", "ptr3", "sca", "scv"]
-              + ["%s%d%d" % (w, d, h) for w in ("x", "y", "t", "l") for d in range(7) for h in range(2)]
-              + ["%s%d" % (w, c) for w in ("veq", "pok", "vo", "voff", "gj") for c in range(len(CH))])
+SEMAPHORES = (["ld1", "ld2", "ld3", "ldown", "ldtok", "ldpar", "ldkv", "ldkw", "sent", "arr1", "arr2", "arr3", "lst", "lst2",
+               "lsent", "st1", "gmr", "gsm", "gmb", "vramp", "vtz", "vc1", "vcc", "vz", "vzb", "vkz", "vcst", "vsel0", "vsel1",
+               "vsel2", "vsel3", "vtok", "vpar", "vpcol", "vhf", "vhx", "vlist", "vpmod", "vpb", "vnb", "vtab", "vd15", "vmcol",
+               "aab", "vgrp", "vm1", "vm2", "vm30", "vm31", "vtgt", "vyb", "aya", "ayb", "afa", "ev0", "ev1", "ev2", "ev3",
+               "ptr0", "ptr1", "ptr2", "ptr3", "sca", "scv"]
+              + ["%s%d%d" % (w, d, h) for w in ("x", "y", "l") for d in range(7) for h in range(2)]
+              + ["%s%d" % (w, c) for w in ("veq", "pok", "voff") for c in range(len(CH))]
+              + ["ag%d" % k for k in range(len(MS))] + ["gj%d" % k for k in range(len(SS))])
+
+
+def meet(a, b):
+    return a[0] < b[1] and b[0] < a[1]
 
 
 def rank_program(g, core, T, topo):
@@ -64,119 +71,135 @@ def rank_program(g, core, T, topo):
     def blk(q):
         return T.best[:, q * 2048:(q + 1) * 2048]
 
-    Y.dma_start(T.snd[:, 0:128], blk((r + 1) % n)).then_inc(S.ld1, 16)
-    A.dma_start(T.part[:], T.par[:]).then_inc(S.ldpar, 16)
+    def tokx(a, b):
+        return T.wv[:, NODE + 1 + a:NODE + 1 + b]
+
+    Y.dma_start(T.snd[0], blk((r + 1) % n)).then_inc(S.ld1, 16)
+    Y.dma_start(T.part[:], T.par[:]).then_inc(S.ldpar, 16)
     Y.dma_start(T.tokc[:], T.tok[:]).then_inc(S.ldtok, 16)
-    A.dma_start(T.snd[:, 128:256], blk((r + 2) % n)).then_inc(S.ld2, 16)
-    Y.dma_start(T.snd[:, 256:384], blk((r + 3) % n)).then_inc(S.ld3, 16)
-    A.dma_start(T.own[:], blk(r)).then_inc(S.ldown, 16)
+    Y.dma_start(T.snd[1], blk((r + 2) % n)).then_inc(S.ld2, 16)
+    Y.dma_start(T.snd[2], blk((r + 3) % n)).then_inc(S.ld3, 16)
+    Y.dma_start(T.own[:], blk(r)).then_inc(S.ldown, 16)
     eng = {k: topo.engines(core, cores[(r + k) % n])[SP[k]] for k in (1, 2, 3)}
     ne = {k: len(eng[k]) for k in eng}
     Y.wait_ge(S.vkz, 2)
     Y.wait_ge(S.sent, sum(ne.values()))
     Y.dma_start(T.kva[:, 17:2065], T.kv[:, mine * 2048:(mine + 1) * 2048]).then_inc(S.ldkv, 16)
-    Y.dma_start(T.kvb[:, 17:2065], T.kv[:, other * 2048:(other + 1) * 2048]).then_inc(S.ldkv, 16)
+    Y.dma_start(T.kvb[:, 17:2065], T.kv[:, other * 2048:(other + 1) * 2048]).then_inc(S.ldkw, 16)
 
     g.iota(T.mb[:], [[-16, 8], [0, 16]], 0, 1, **low).then_inc(S.gmb, 1)
-    g.iota(T.sm[:], [[-1, 32]], 0, 1).then_inc(S.gsm, 1)
-    g.iota(T.mr[:], [[0, 8], [-4096, 16]], 0, 0, **low).then_inc(S.gmr, 1)
+    g.iota(T.sm[:], [[-1, 16]], 0, 1).then_inc(S.gsm, 1)
     for k in (1, 2, 3):
-        dst = cores[(r + k) % n]
-        rid, pid = topo.addr(dst, core)
+        rid, pid = topo.addr(cores[(r + k) % n], core)
         g.wait_ge(S["ld%d" % k], 16)
-        g.remote_dma(T["land%d" % k][:], T.snd[:, (k - 1) * 128:k * 128], S["arr%d" % k], S.sent, pid, rid,
-                     sum(1 << e for e in eng[k]))
-    g.iota(T.wi[:], [[1, 144]], -15, -1, **low).then_inc(S.gwi, 1)
-    g.iota(T.c16r[:], [[16, 128]], 0, 0, **low).then_inc(S.gpre, 1)
-    for c, (c0, c1) in enumerate(CH):
-        g.iota(T.jrow[:, 16 * c0 - 64:16 * c1 - 64], [[1, 16 * (c1 - c0)]], 16 * c0 + 1, 0, **low).then_inc(S["gj%d" % c], 1)
+        g.remote_dma(T["land%d" % k][:], T.snd[k - 1], S["arr%d" % k], S.sent, pid, rid, sum(1 << e for e in eng[k]))
+    g.iota(T.mr[0:32, :], [[0, 8], [1, 16]], 0, 0, **low).then_inc(S.gmr, 1)
+    jr = [0]
+    for k, (a, b) in enumerate(SS):
+        w = 16 * max([b - a] + [y - x for x, y in SV if k == 0])
+        g.iota(T.jrow[:, jr[k]:jr[k] + w], [[1, w]], 16 * a + 1, 0, **low).then_inc(S["gj%d" % k], 1)
+        jr.append(jr[k] + w)
+
+    def sels(a0, a1):
+        for a in range(a0, a1):
+            V.tensor_scalar(T.sel[:, 128 * a:128 * a + 128], T.mb[:], float(a), None, Op.is_equal).then_inc(S["vsel%d" % (a // 4)], 1)
+
+    def weight(k):
+        if k == 3:
+            V.tensor_scalar(T.c1[:], T.d15[:], 0.0, W, Op.is_equal, Op.mult).then_inc(S.vc1, 1)
+        elif k == 2:
+            V.tensor_scalar(T.c2[:], T.d15[:], 1.0, None, Op.not_equal).then_inc(S.vc1, 1)
+        elif k == 1:
+            V.tensor_scalar(T.cc[:, 31:32], T.pmod[:], 15.0, 1.0 / W, Op.is_equal, Op.max).then_inc(S.vcc, 1)
+        else:
+            V.wait_ge(S.vc1, 2)
+            V.tensor_tensor(T.cc[:, 1:31:2], T.c1[:, 0:15], T.c2[:, 0:15], Op.max).then_inc(S.vcc, 1)
 
     V.memset(T.zero[:], 0.0).then_inc(S.vz, 1)
+    V.memset(T.tab[:], 0.0).then_inc(S.vtz, 1)
     V.wait_ge(S.gmb, 1)
-    for a in range(16):
-        V.tensor_scalar(T.sel[:, 128 * a:128 * a + 128], T.mb[:], float(a), None, Op.is_equal).then_inc(S.vsel, 1)
+    sels(0, 4)
     V.wait_ge(S.gsm, 1)
     V.tensor_scalar(T.d15[:], T.sm[:], 15, None, Op.bitwise_and).then_inc(S.vd15, 1)
-    V.wait_ge(S.gmr, 1)
-    V.tensor_copy(T.mrf[:], T.mr[:]).then_inc(S.vmr, 1)
-    V.wait_ge(S.aab, 1)
-    V.tensor_scalar(T.grp[:], T.ab[:], 8.0, 2048.0, Op.is_lt, Op.mult).then_inc(S.vgrp, 1)
+    sels(4, 8)
     V.wait_ge(S.vd15, 1)
-    V.tensor_scalar(T.msk[:], T.d15[:], 0.0, None, Op.is_equal).then_inc(S.vmsk, 1)
-    V.tensor_scalar(T.mcol[:], T.d15[:, 0:16], 0.0, None, Op.is_equal).then_inc(S.vmcol, 1)
+    V.tensor_scalar(T.mcol[:], T.d15[:], 0.0, None, Op.is_equal).then_inc(S.vmcol, 1)
     V.tensor_copy(T.pmod[:], T.d15[:, 0:1]).then_inc(S.vpmod, 1)
-    V.memset(T.cst[:], 2.0 ** -19).then_inc(S.vcst, 1)
-    V.memset(T.cc[:, 1:64:2], 1.0).then_inc(S.vcc, 1)
-    V.memset(T.kva[:, 16:32], 0.0).then_inc(S.vkz, 1)
-    V.memset(T.kvb[:, 16:32], 0.0).then_inc(S.vkz, 1)
-    V.wait_ge(S.vpmod, 1)
-    V.tensor_scalar(T.pb[:], T.pmod[:], -4096.0, 2048.0, Op.mult, Op.add).then_inc(S.vpb, 1)
-    V.tensor_scalar(T.qc[:], T.pmod[:], -1.0 / 4096, (NODE + 1) / 4096, Op.mult, Op.add).then_inc(S.vqc, 1)
+    V.wait_ge(S.aab, 1)
+    V.tensor_scalar(T.grp[:], T.ab[:], 8.0, 4096.0, Op.is_lt, Op.mult).then_inc(S.vgrp, 1)
     V.wait_ge(S.ldpar, 16)
-    V.tensor_scalar(T.parhi[:], T.part[:], 7, None, Op.arith_shift_right).then_inc(S.vhi, 1)
+    V.tensor_scalar(T.hif[:], T.part[:], 1.0 / 128, HI - 63.5 / 128, Op.mult, Op.add).then_inc(S.vhf, 1)
     V.wait_ge(S.ldtok, 16)
     V.tensor_scalar(T.tokf[:], T.tokc[:], -2048.0, None, Op.add).then_inc(S.vtok, 1)
-    V.wait_ge(S.vhi, 1)
-    V.tensor_scalar(T.hif[:], T.parhi[:], 2.0, None, Op.mult).then_inc(S.vhf, 1)
-    V.tensor_scalar(T.parlo[:], T.part[:], 127, None, Op.bitwise_and).then_inc(S.vpar, 1)
     V.wait_ge(S.vmcol, 1)
     V.wait_ge(S.vhf, 1)
-    for i in range(HV):
+    for i in range(16):
         V.tensor_scalar(T.hx[:, i:2048:16], T.hif[:], T.mcol[:, i:i + 1], None, Op.mult).then_inc(S.vhx, 1)
-    V.memset(T.ww[:, ZA:ZB], 0.0).then_inc(S.vzb, 1)
-
-    def offs(b):
-        P.matmul(T["tr%d" % b][:, 0:512], T.mrf[:], T.sel[:, 0:512], True, False).then_inc(S["ptr%d" % b], 1)
+    V.wait_ge(S.vpmod, 1)
+    V.tensor_scalar(T.pb[:], T.pmod[:], -4096.0, 2048.0 - 4096.0 * HI, Op.mult, Op.add).then_inc(S.vpb, 1)
+    sels(8, 16)
+    V.tensor_scalar(T.nb[:], T.pmod[:], 4096.0, 4096.0 * HI - 2048.0, Op.mult, Op.add).then_inc(S.vnb, 1)
+    V.memset(T.cst[:], 0.25).then_inc(S.vcst, 1)
+    V.memset(T.kva[:, 16:32], 0.0).then_inc(S.vkz, 1)
+    V.memset(T.kvb[:, 16:32], 0.0).then_inc(S.vkz, 1)
+    V.wait_ge(S.vcst, 1)
+    V.tensor_tensor_scan(T.c16r[:], T.cst[:], T.cst[:], -0.5, Op.add, Op.add).then_inc(S.vramp, 1)
+    V.wait_ge(S.vtz, 1)
+    V.tensor_scalar(T.tab[:, 15:143:16], T.ab[:, 0:128:16], 8.0, 4096.0, Op.is_lt, Op.mult).then_inc(S.vtab, 1)
+    V.tensor_scalar(T.parlo[:], T.part[:], 127, None, Op.bitwise_and).then_inc(S.vpar, 1)
+    V.memset(T.cc[:, 0:32:2], 1.0).then_inc(S.vcc, 1)
+    V.memset(T.wv[:, NODE:NODE + 1], 0.0).then_inc(S.vzb, 1)
+    for k in (3, 2, 1, 0):
+        if "f%d" % k not in ORDER:
+            weight(k)
 
     def toks(b):
+        P.wait_ge(S["vsel%d" % b], 4)
         for k in range(4):
             a = 4 * b + k
-            P.matmul(T["tr%d" % b][:, 128 * k:128 * k + 128], T.sel[:, 128 * a:128 * a + 128], T.tokf[:], False,
+            P.matmul(T["tr%d" % b][:, 128 * k:128 * k + 128], T.sel[:, 128 * a:128 * a + 128], T.tokf[:], b < 2 and k == 0,
                      b > 1 and k == 3).then_inc(S["ptr%d" % b], 1)
 
     def places(b):
         P.matmul(T["tr%d" % b][:, 0:512], T.grp[:], T.hx[:, 512 * b:512 * b + 512], b > 1, b < 2).then_inc(S["ptr%d" % b], 1)
 
-    P.wait_ge(S.vsel, 16)
-    P.wait_ge(S.vmr, 1)
-    offs(0)
-    offs(1)
     P.wait_ge(S.vtok, 1)
     toks(0)
     toks(1)
     P.wait_ge(S.vgrp, 1)
-    P.wait_ge(S.vhx, HV)
-    P.wait_ge(S.ahx, 16 - HV)
+    P.wait_ge(S.vhx, 16)
     places(0)
     places(1)
     for b in (2, 3):
         places(b)
         toks(b)
-    P.wait_ge(S.vcst, 1)
-    P.wait_ge(S.gpre, 1)
+    P.wait_ge(S.vramp, 1)
+    P.wait_ge(S.gmr, 1)
     for c, (c0, c1) in enumerate(CH):
         P.matmul(ps[c][:, 0:c1 - c0], T.cst[:], T.c16r[:, c0:c1], True, False).then_inc(S["pok%d" % c], 1)
+        P.matmul(ps[c][:, 0:c1 - c0], T.mr[0:4, :], T.cst[0:4, c0:c1], False, False).then_inc(S["pok%d" % c], 1)
     P.wait_ge(S.vtab, 1)
 
-    def zeros(b, k0, k1, sem):
+    def zeros(k0, k1):
         for k in range(k0, k1):
-            A.activation(T.ww[:, b + ZC * k:b + ZC * k + ZC], T.zero[:], Fn.Silu).then_inc(sem, 1)
+            A.activation(T.ww[:, NODE + ZC * k:NODE + ZC * k + ZC], T.zero[:], Fn.Silu).then_inc(S.afa, 1)
 
     A.wait_ge(S.gmb, 1)
     A.activation(T.ab[:], T.mb[:], Fn.Abs, bias=-7.5).then_inc(S.aab, 1)
     A.wait_ge(S.vz, 1)
-    zeros(NODE, 0, Z0, S.afa)
-    A.wait_ge(S.vmsk, 1)
-    A.wait_ge(S.vhf, 1)
-    for i in range(HV, 16):
-        A.activation(T.hx[:, i:2048:16], T.hif[:], Fn.Copy, scale=T.msk[:, i:i + 1]).then_inc(S.ahx, 1)
-    zeros(NODE, Z0, NZ, S.afa)
+    zeros(0, ZR[0])
     A.wait_ge(S.vpb, 1)
+    nev = [0] * 4
     for b in range(4):
-        A.wait_ge(S["ptr%d" % b], 6 if b < 2 else 5)
-        A.activation(T.tokx[:, 512 * b:512 * b + 512], T["tr%d" % b][:], Fn.Identity, bias=2048.0 if b < 2 else T.pb[:]).then_inc(
-            S["ev%d" % b], 1)
-        zeros(MID + NODE, ZR[b], ZR[b + 1], S.afb)
+        cols = [x for x in range(32 * b, 32 * b + 32) if not any(meet((x, x + 1), m) for m in MS)]
+        for x in cols:
+            if x - 1 not in cols:
+                y = min(z for z in range(x, 32 * b + 33) if z not in cols)
+                A.wait_ge(S["ptr%d" % b], 5)
+                A.activation(tokx(16 * x, 16 * y), T["tr%d" % b][:, 16 * x - 512 * b:16 * y - 512 * b], Fn.Identity,
+                             bias=T.pb[:]).then_inc(S["ev%d" % b], 1)
+                nev[b] += 1
+        zeros(ZR[b], ZR[b + 1])
 
     V.wait_ge(S.ldown, 16)
     prev = T.own[:, 0:128]
@@ -185,11 +208,10 @@ def rank_program(g, core, T, topo):
         V.wait_ge(S["arr%d" % k], ne[k])
         V.tensor_tensor(m, prev, T["land%d" % k][:], Op.max).then_inc(S["vm%d" % k], 1)
         if k == 1:
-            V.wait_ge(S.gwi, 1)
-            V.tensor_scalar(T.tab[:], T.wi[:], T.pmod[:], 0.0, Op.add, Op.is_equal).then_inc(S.vtab, 1)
-        else:
             V.wait_ge(S.vpar, 1)
             V.tensor_copy(T.lo[:], T.parlo[:]).then_inc(S.vlist, 1)
+        else:
+            V.tensor_scalar(T.pcol[:], T.part[:], NODE + 1.0, None, Op.add).then_inc(S.vpcol, 1)
         V.wait_ge(S["vm%d" % k], 1)
         prev = m
     V.wait_ge(S.arr3, ne[3])
@@ -199,127 +221,146 @@ def rank_program(g, core, T, topo):
     for h in range(2):
         V.wait_ge(S["vm3%d" % h], 1)
         V.tensor_scalar(T.tgt[:, 64 * h:64 * h + 64], T.mx[:, 64 * h:64 * h + 64], 4095, None, Op.bitwise_and).then_inc(S.vtgt, 1)
-    V.wait_ge(S.vqc, 1)
-    V.tensor_scalar(T.pcol[:], T.part[:], 1.0 / 4096, T.qc[:], Op.mult, Op.add).then_inc(S.vpcol, 1)
-    V.wait_ge(S.vlist, 1)
-    V.wait_ge(S.vtgt, 2)
+    for q in (V, A):
+        q.wait_ge(S.vlist, 1)
+        q.wait_ge(S.vtgt, 2)
+    A.wait_ge(S.vnb, 1)
+    V.wait_ge(S.vpcol, 1)
 
-    def match(c):
-        c0, c1 = CH[c]
-        for b in range(4):
-            if c0 < 32 * b + 32 and c1 > 32 * b:
-                V.wait_ge(S["ev%d" % b], 1)
-        V.tensor_tensor(T.eq[:, 16 * c0:16 * c1], T.tgt[:, 0:128].indirect(T.lo[:, c0:c1]), T.tokx[:, 16 * c0:16 * c1],
-                        Op.is_equal).then_inc(S["veq%d" % c], 1)
-        P.wait_ge(S["veq%d" % c], 1)
+    neq = [sum(meet(m, ch) for m in MV + MS) for ch in CH]
+
+    def piece(m):
+        return S["veq%d" % [meet(m, ch) for ch in CH].index(True)]
+
+    def rows_out(a, b):
+        for k in range(a // 32, (b + 31) // 32):
+            if nev[k]:
+                V.wait_ge(S["ev%d" % k], nev[k])
+
+    def match(k):
+        a, b = MV[k]
+        rows_out(a, b)
+        V.tensor_tensor(T.eq[:, 16 * a:16 * b], T.tgt[:, 0:128].indirect(T.lo[:, a:b]), tokx(16 * a, 16 * b),
+                        Op.is_equal).then_inc(piece(MV[k]), 1)
+
+    def compare(k):
+        a, b = MS[k]
+        u = a // 32
+        rows_out(a, b)
+        V.wait_ge(S["ptr%d" % u], 5)
+        V.wait_ge(S["ag%d" % k], 1)
+        V.tensor_tensor(T.eq[:, 16 * a:16 * b], tokx(16 * a, 16 * b), T["tr%d" % u][:, 16 * a - 512 * u:16 * b - 512 * u],
+                        Op.is_equal).then_inc(piece(MS[k]), 1)
+
+    for k, (a, b) in enumerate(MS):
+        A.activation(tokx(16 * a, 16 * b), T.tgt[:, 0:128].indirect(T.lo[:, a:b]), Fn.Identity, bias=T.nb[:]).then_inc(
+            S["ag%d" % k], 1)
+    for c, (c0, c1) in enumerate(CH):
+        P.wait_ge(S["veq%d" % c], neq[c])
         for i in range(16):
             P.matmul(ps[c][:, 0:c1 - c0], T.tab[:, 15 - i:143 - i], T.eq[:, 16 * c0 + i:16 * c1:16],
                      False, i == 15).then_inc(S["pok%d" % c], 1)
 
     def offsets(c):
         c0, c1 = CH[c]
-        V.wait_ge(S.vpcol, 1)
-        V.wait_ge(S["pok%d" % c], 17)
-        V.tensor_tensor(T.offi[:, c0:c1], ps[c][:, 0:c1 - c0], T.pcol[:, c0:c1], Op.min).then_inc(S["vo%d" % c], 1)
-        if c == 0:
-            V.tensor_scalar(T.c1[:], T.d15[:], 15.0, W, Op.is_equal, Op.mult).then_inc(S.vc1, 1)
-            V.tensor_scalar(T.c2[:], T.d15[:], 1.0, None, Op.min).then_inc(S.vc1, 1)
-        elif c == 1:
-            V.memset(T.ww[:, ZB:2 * MID], 0.0).then_inc(S.vzb, 1)
+        V.wait_ge(S["pok%d" % c], 18)
+        V.tensor_tensor(T.off[:, c0:c1], ps[c][:, 0:c1 - c0], T.pcol[:, c0:c1], Op.min).then_inc(S["voff%d" % c], 1)
+
+    def offsets_for(q, m):
+        for c, ch in enumerate(CH):
+            if meet(m, ch):
+                q.wait_ge(S["voff%d" % c], 1)
+
+    def scatter(k):
+        a, b = SV[k]
+        if k:
+            V.wait_ge(S.scv, k)
         else:
-            V.tensor_scalar(T.sc[:], T.pmod[:], 15.0, 1.0 / W, Op.is_equal, Op.max).then_inc(S.vsc, 1)
-            V.wait_ge(S.vc1, 2)
-            V.tensor_tensor(T.cc[:, 0:64:2], T.c1[:], T.c2[:], Op.max).then_inc(S.vcc, 1)
-        V.wait_ge(S["vo%d" % c], 1)
-        V.tensor_scalar(T.off[:, c0:c1], T.offi[:, c0:c1], 4096.0, T.pmod[:], Op.mult, Op.add).then_inc(S["voff%d" % c], 1)
+            V.wait_ge(S.vzb, 1)
+            V.wait_ge(S.gj0, 1)
+            for c in range(len(CH)):
+                V.wait_ge(S["veq%d" % c], neq[c])
+        offsets_for(V, SV[k])
+        V.tensor_scalar(T.wv[:].indirect(T.off[:, a:b]), T.jrow[:, 0:16 * (b - a)], BIG, 16 * (a - SS[0][0]) * BIG,
+                        Op.mult, Op.add).then_inc(S.scv, 1)
 
-    match(0)
-    match(1)
-    offsets(0)
-    match(2)
-    offsets(1)
+    for w in ORDER.split():
+        {"v": match, "c": compare, "o": offsets, "s": scatter, "f": weight}[w[0]](int(w[1]))
     A.wait_ge(S.afa, NZ)
-    for k, c in enumerate((0, 2)):
-        c0, c1 = CH[c]
-        A.wait_ge(S["gj%d" % c], 1)
-        A.wait_ge(S["voff%d" % c], 1)
+    for k, (a, b) in enumerate(SS):
+        A.wait_ge(S["gj%d" % k], 1)
+        offsets_for(A, SS[k])
         if k:
-            A.wait_ge(S.sca, 1)
-        A.activation(T.ww[:, 0:MID].indirect(T.off[:, c0:c1]), T.jrow[:, 16 * c0 - 64:16 * c1 - 64], Fn.Silu).then_inc(S.sca, 1)
-    V.wait_ge(S.vzb, 2)
-    V.wait_ge(S.afb, ZR[4])
-    V.wait_ge(S.gj1, 1)
-    V.wait_ge(S.voff1, 1)
-    for k, (c0, c1) in enumerate(((CH[1][0], VS), (VS, CH[1][1]))):
-        if k:
-            offsets(2)
-            V.wait_ge(S.scv, 1)
-        V.tensor_copy(T.ww[:, MID:2 * MID].indirect(T.off[:, c0:c1]), T.jrow[:, 16 * c0 - 64:16 * c1 - 64]).then_inc(S.scv, 1)
+            A.wait_ge(S.sca, k)
+        A.activation(T.ww[:].indirect(T.off[:, a:b]), T.jrow[:, jr[k]:jr[k] + 16 * (b - a)], Fn.Silu).then_inc(S.sca, 1)
 
-    def look(q, d, w):
-        w0 = (NODE, MID + NODE)[w]
-        for h in range(2 if d else 1):
-            e0, b = 128 * d + 64 * h, 4 * d + 2 * h
-            if d:
-                q.wait_ge(S["l%d%d" % (d - 1, h)], 1)
-                src, out = T.ww[:, w0:w0 + REG].indirect(T.ls[:, b:b + 2]), T.vs[:, e0 + w:e0 + 64:2]
-            else:
-                src, out = T.ww[:, w0 + 1:w0 + 65], T.vs[:, w:128:2]
-            if w:
-                q.tensor_copy(out, src).then_inc(S["y%d%d" % (d, h)], 1)
-            else:
-                q.activation(out, src, Fn.Copy).then_inc(S["x%d%d" % (d, h)], 1)
+    def look(q, d, h):
+        w = int(q is V)
+        win = (T.ww, T.wv)[w]
+        e0, b = 128 * d + 64 * h, LS + 28 - 4 * d + 2 * h
+        if d:
+            q.wait_ge(S["l%d%d" % (d - 1, h)], 2)
+            src, out = win[:, NODE:NODE + REG].indirect(T.ls[:, b:b + 2]), T.vs[:, e0 + w:e0 + 64:2]
+        elif h:
+            return
+        else:
+            src, out = win[:, NODE + 1:NODE + 65], T.vs[:, w:128:2]
+        if w:
+            q.tensor_scalar(out, src, 1.0 / BIG, 0.25, Op.mult, Op.add).then_inc(S["y%d%d" % (d, h)], 1)
+        else:
+            q.activation(out, src, Fn.Copy).then_inc(S["x%d%d" % (d, h)], 1)
 
-    V.wait_ge(S.scv, 2)
+    def scans(d, h):
+        for w in "yx":
+            V.wait_ge(S["%s%d%d" % (w, d, h if d else 0)], 1)
+        for c in (2 * h, 2 * h + 1):
+            b = 24 - 4 * d + c
+            V.tensor_tensor_scan(T.ls[:, b:b + LS + 1:4], T.vs[:, 128 * d + 32 * c:128 * d + 32 * c + 32], T.cc[:], 0.0,
+                                 Op.add, Op.mult).then_inc(S["l%d%d" % (d, h)], 1)
+
+    V.wait_ge(S.scv, len(SV))
+    V.wait_ge(S.vcc, 3)
     for d in range(7):
-        look(V, d, 1)
-        if d == 0:
-            V.wait_ge(S.vcc, 2)
-            V.wait_ge(S.vsc, 1)
-        for h in range(2):
-            e0 = 128 * d + 64 * h
-            for w in "yx":
-                V.wait_ge(S["%s%d%d" % (w, d, h if d else 0)], 1)
-            V.tensor_tensor_scan(T.ts[:, e0:e0 + 64], T.cc[:], T.vs[:, e0:e0 + 64], 0.0, Op.mult, Op.add).then_inc(
-                S["t%d%d" % (d, h)], 1)
-        for h in range(2):
-            e0, b = 128 * d + 64 * h, 4 * d + 4 + 2 * h
-            V.wait_ge(S["t%d%d" % (d, h)], 1)
-            V.tensor_scalar(T.ls[:, b:b + 2], T.ts[:, e0 + 31:e0 + 64:32], T.sc[:], 0.25, Op.mult, Op.add).then_inc(
-                S["l%d%d" % (d, h)], 1)
+        for step in (lambda h: look(V, d, h), lambda h: scans(d, h)):
+            step(0)
+            step(1)
 
     def list_of(q, d):
-        q.wait_ge(S["l%d0" % (d - 1)], 1)
-        q.wait_ge(S["l%d1" % (d - 1)], 1)
+        q.wait_ge(S["l%d0" % (d - 1)], 2)
+        q.wait_ge(S["l%d1" % (d - 1)], 2)
 
     dst = cores[mate]
     rid, pid = topo.addr(dst, core)
     nl = len(topo.engines(core, dst))
-    m = 4 * EARLY + 4
+    m = 28 - 4 * EARLY
     for d in range(1, EARLY + 1):
         list_of(g, d)
-    g.remote_dma(T.k2[:, 4:m], T.ls[:, 4:m], S.lst, S.lsent, pid, rid, topo.mask(core, dst))
+    g.remote_dma(T.k2[:, m:28], T.ls[:, LS + m:LS + 28], S.lst, S.lsent, pid, rid, topo.mask(core, dst))
     for d in range(EARLY + 1, 8):
         list_of(g, d)
-    g.remote_dma(T.k2[:, m:32], T.ls[:, m:32], S.lst2, S.lsent, pid, rid, topo.mask(core, dst))
+    g.remote_dma(T.k2[:, 0:m], T.ls[:, LS:LS + m], S.lst2, S.lsent, pid, rid, topo.mask(core, dst))
     g.wait_ge(S.lsent, 2 * nl)
     ka, kb = T.kva[:, 16:2065], T.kvb[:, 16:2065]
-    A.wait_ge(S.sca, 2)
+    A.wait_ge(S.sca, len(SS))
     for d in range(8):
         if d < 7:
             look(A, d, 0)
+            look(A, d, 1)
         else:
             list_of(A, d)
         if d == 0:
-            A.wait_ge(S.ldkv, 32)
-        A.activation(T.ya[:, d:512:8], ka.indirect(T.ls[:, 4 * d:4 * d + 4]) if d else T.kva[:, 17:81], Fn.Copy).then_inc(S.aya, 1)
+            A.wait_ge(S.ldkv, 16)
+        src = ka.indirect(T.ls[:, LS + 28 - 4 * d:LS + 32 - 4 * d]) if d else T.kva[:, 17:81]
+        A.activation(T.ya[:, d:512:8], src, Fn.Copy).then_inc(S.aya, 1)
     Y.wait_ge(S.aya, 8)
+    Y.wait_ge(S.lsent, 2 * nl)
     Y.dma_start(T.y[:, 512 * mine:512 * mine + 512], T.ya[:]).then_inc(S.st1, 16)
-    V.wait_ge(S.ldkv, 32)
+    V.wait_ge(S.ldkw, 16)
+    A.wait_ge(S.ldkw, 16)
     V.tensor_copy(T.yb[:, 0:512:8], T.kvb[:, 17:81]).then_inc(S.vyb, 1)
 
     def keys(d, v):
-        out, src = T.yb[:, d:512:8], kb.indirect(T.k2[:, 4 * d:4 * d + 4])
+        out, src = T.yb[:, d:512:8], kb.indirect(T.k2[:, 28 - 4 * d:32 - 4 * d])
         if v:
             V.tensor_copy(out, src).then_inc(S.vyb, 1)
         else:

@@ -1,22 +1,23 @@
 from concourse.mybir import AluOpType as Op, ActivationFunctionType as Fn
 
-CH = [(4, 42), (42, 96), (96, 128)]
-MV = [(4, 42), (42, 52)]
-MS = [(52, 64), (64, 96), (96, 128)]
-SS = [(4, 42), (96, 128)]
-SV = [(42, 56), (56, 96)]
-ORDER = "v0 v1 c0 c1 o0 c2 o1 f0 s0 o2 s1"
+CH = [(4, 48), (48, 96), (96, 128)]
+MV = [(4, 26), (26, 48), (48, 64)]
+MS = [(64, 96), (96, 128)]
+LATE = 96
+SS = [(4, 34), (94, 128)]
+SV = [(34, 48), (48, 94)]
+ORDER = "v0 v1 v2 c0 o0 c1 s0 o1 f2 o2 s1"
 NODE, REG = 2048, 2049
 BIG = 2.0 ** 30
 ZC = 257
 NZ = 8
-ZR = (2, 2, 2, 3, 8)
-LS = 124
+Z0, Z1 = 4, 8
+LS = 160
 HI = 144.0
 SP = {1: slice(0, None, 2), 2: slice(1, None, 2), 3: slice(0, None)}
 W = 2.0 ** 24
-EARLY = 5
-KV1, KV2 = (1, 2), (6,)
+KIN, KVO = (2, 4, 6), (1, 3)
+KV1 = (1, 2, 3)
 
 I32 = ("sbuf", [128, 128], "int32")
 U16 = ("sbuf", [128, 128], "uint16")
@@ -31,24 +32,24 @@ def sb(k, d="float32"):
 
 SCRATCH = {
     "own": I32, "snd": ("dram", [3, 128, 128], "int32"), "land1": I32, "land2": I32, "land3": I32, "mx": I32, "tgt": I32,
-    "tokc": I32, "tokf": F16, "part": I32, "parlo": I32, "lo": U16, "hif": B16, "pcol": sb(128),
+    "tokc": I32, "tokf": F16, "part": I32, "parlo": I32, "parf": F16, "lo": U16, "hif": B16, "pcol": sb(128),
     "sm": sb(16, "int32"), "d15": sb(16, "int32"), "pmod": sb(1), "pb": sb(1), "nb": sb(1), "mb": B16, "ab": B16,
-    "grp": B16, "mcol": sb(16, "bfloat16"), "hx": sb(2048, "bfloat16"),
-    "sel": sb(2048, "float16"), "tab": sb(144, "float16"), "cst": B16, "mr": B16,
-    "c16r": B16, "cc": sb(32), "c1": sb(16), "c2": sb(16), "jrow": sb(2048),
-    "eq": sb(2048, "float16"), "off": U16, "zero": sb(ZC), "ww": sb(NODE + NZ * ZC), "wv": sb(NODE + REG),
-    "vs": sb(896), "ls": sb(LS + 32, "uint16"), "k2": sb(32, "uint16"),
+    "grp": B16, "mcol": sb(16, "bfloat16"), "hx": sb(2048, "bfloat16"), "half": sb(2), "dw": sb(144, "bfloat16"),
+    "idw": sb(288, "float16"), "sel": sb(2048, "float16"), "tab": sb(144, "float16"), "cst": B16, "mr": B16, "c16r": B16,
+    "cc": sb(33), "c1": sb(16), "c2": sb(16), "wa": sb(16), "wb": sb(16), "ra": sb(64), "jrow": sb(2048),
+    "eq": sb(2048, "float16"), "off": U16, "gx": sb(16 * (128 - LATE)), "zero": sb(ZC), "ww": sb(NODE + NZ * ZC),
+    "wv": sb(NODE + REG), "vs": sb(792), "ls": sb(LS + 64, "uint16"), "k2": sb(64, "uint16"),
     "kva": sb(2080, "bfloat16"), "kvb": sb(2080, "bfloat16"), "ya": sb(512, "bfloat16"), "yb": sb(512, "bfloat16"),
     "tr0": PS, "tr1": PS, "tr2": PS, "tr3": PS, "ps0": PS, "ps1": PS, "ps2": PS, "pm": PS,
 }
 SEMAPHORES = (["ld1", "ld2", "ld3", "ldown", "ldtok", "ldpar", "ldkv", "ldkw", "sent", "arr1", "arr2", "arr3", "lst", "lst2",
-               "lsent", "st1", "gmr", "gsm", "gmb", "vramp", "vtz", "vc1", "vcc", "vz", "vzb", "vkz", "vcst", "vsel0", "vsel1",
-               "vsel2", "vsel3", "vtok", "vpar", "vpcol", "vhf", "vhx", "vlist", "vpmod", "vpb", "vnb", "vtab", "vd15", "vmcol",
-               "aab", "vgrp", "vm1", "vm2", "vm30", "vm31", "vtgt", "vyb", "aya", "ayb", "afa", "ev0", "ev1", "ev2", "ev3",
-               "ptr0", "ptr1", "ptr2", "ptr3", "sca", "scv"]
-              + ["%s%d%d" % (w, d, h) for w in ("x", "y", "l") for d in range(7) for h in range(2)]
-              + ["%s%d" % (w, c) for w in ("veq", "pok", "voff") for c in range(len(CH))]
-              + ["ag%d" % k for k in range(len(MS))] + ["gj%d" % k for k in range(len(SS))])
+               "lsent", "st1", "gmr", "gsm", "gmb", "gdw", "gj0", "gj1", "gj2", "vramp", "vtz", "vc1", "vc3", "vcc", "vz", "vzb",
+               "vkz", "vcst", "vtok", "vpar", "vpcol", "vhf", "vhx", "vlist", "vpmod", "vpb", "vnb", "vtab", "vd15", "vmcol",
+               "vhalf", "vidw", "vgrp", "vm1", "vm2", "vm30", "vm31", "vtgt", "aab", "aown", "glz", "apc", "afa", "ppar",
+               "sca", "scv", "lfix", "ya", "yb"]
+              + ["%s%d" % (w, c) for w in ("vsel", "ev", "ptr", "veq", "ra", "x", "y") for c in range(4)]
+              + ["%s%d" % (w, c) for w in ("pok", "voff") for c in range(len(CH))] + ["ag%d" % k for k in range(len(MS))]
+              + ["l%d%d" % (d, c) for d in range(7) for c in range(4)])
 
 
 def meet(a, b):
@@ -67,6 +68,8 @@ def rank_program(g, core, T, topo):
     mine, other = r // 2, 1 - r // 2
     low = {"allow_small_or_imprecise_dtypes": True}
     ps = [T.ps0, T.ps1, T.ps2]
+    C0, C1 = CH[0]
+    K0 = C1 - C0
 
     def blk(q):
         return T.best[:, q * 2048:(q + 1) * 2048]
@@ -93,30 +96,43 @@ def rank_program(g, core, T, topo):
         rid, pid = topo.addr(cores[(r + k) % n], core)
         g.wait_ge(S["ld%d" % k], 16)
         g.remote_dma(T["land%d" % k][:], T.snd[k - 1], S["arr%d" % k], S.sent, pid, rid, sum(1 << e for e in eng[k]))
+    g.iota(T.dw[:], [[1, 144]], -8, -1, **low).then_inc(S.gdw, 1)
     g.iota(T.mr[0:32, :], [[0, 8], [1, 16]], 0, 0, **low).then_inc(S.gmr, 1)
-    jr = [0]
-    for k, (a, b) in enumerate(SS):
-        w = 16 * max([b - a] + [y - x for x, y in SV if k == 0])
-        g.iota(T.jrow[:, jr[k]:jr[k] + w], [[1, w]], 16 * a + 1, 0, **low).then_inc(S["gj%d" % k], 1)
-        jr.append(jr[k] + w)
+    for k, (a, b) in enumerate((SS[0], SV[0])):
+        g.iota(T.jrow[:, 16 * a:16 * b], [[8, b - a], [8 * K0, 2], [1, 8]], 16 * C0 + 8 * (a - C0) + 1, 0, **low).then_inc(
+            S["gj%d" % k], 1)
+    g.iota(tokx(16 * LATE, 2048), [[0, 2048 - 16 * LATE]], 0, 0, **low).then_inc(S.glz, 1)
+    nj = 16 * max(b - a for a, b in (SS[1], SV[1]))
+    g.iota(T.jrow[:, 16 * C1:16 * C1 + nj], [[1, nj]], 16 * SS[1][0] + 1, 0, **low).then_inc(S.gj2, 1)
 
     def sels(a0, a1):
         for a in range(a0, a1):
             V.tensor_scalar(T.sel[:, 128 * a:128 * a + 128], T.mb[:], float(a), None, Op.is_equal).then_inc(S["vsel%d" % (a // 4)], 1)
 
-    def weight(k):
-        if k == 3:
+    def tables(k):
+        if k == 0:
             V.tensor_scalar(T.c1[:], T.d15[:], 0.0, W, Op.is_equal, Op.mult).then_inc(S.vc1, 1)
-        elif k == 2:
             V.tensor_scalar(T.c2[:], T.d15[:], 1.0, None, Op.not_equal).then_inc(S.vc1, 1)
         elif k == 1:
-            V.tensor_scalar(T.cc[:, 31:32], T.pmod[:], 15.0, 1.0 / W, Op.is_equal, Op.max).then_inc(S.vcc, 1)
-        else:
+            V.tensor_scalar(T.cc[:, 31:32], T.pmod[:], 15.0, 1.0 / W, Op.is_equal, Op.max).then_inc(S.vc3, 1)
             V.wait_ge(S.vc1, 2)
+            V.tensor_tensor(T.wa[:], T.c1[:], T.c2[:], Op.max).then_inc(S.vc3, 1)
             V.tensor_tensor(T.cc[:, 1:31:2], T.c1[:, 0:15], T.c2[:, 0:15], Op.max).then_inc(S.vcc, 1)
+        elif k == 2:
+            V.wait_ge(S.vc3, 2)
+            V.tensor_scalar(T.wb[:, 0:15], T.wa[:, 0:15], 1.0 / W, None, Op.max).then_inc(S.vcc, 1)
+            V.tensor_scalar(T.wa[:, 15:16], T.wa[:, 15:16], 1.0 / W, BIG, Op.max, Op.mult).then_inc(S.vcc, 1)
+            A.wait_ge(S.vc3, 2)
+            A.activation(T.wb[:, 15:16], T.cc[:, 31:32], Fn.Copy, scale=(1 + 2.0 ** -13) / BIG).then_inc(S.vcc, 1)
+        else:
+            V.memset(T.wv[:, NODE:NODE + 1], 0.0).then_inc(S.vzb, 1)
+            V.memset(T.cc[:, 0:33:2], 1.0).then_inc(S.vcc, 1)
+            V.memset(T.vs[:, 32:792:33], 0.0).then_inc(S.vcc, 1)
+            V.memset(T.ls[:, LS:LS + 64], 0).then_inc(S.vcc, 1)
 
     V.memset(T.zero[:], 0.0).then_inc(S.vz, 1)
     V.memset(T.tab[:], 0.0).then_inc(S.vtz, 1)
+    tables(3)
     V.wait_ge(S.gmb, 1)
     sels(0, 4)
     V.wait_ge(S.gsm, 1)
@@ -138,20 +154,21 @@ def rank_program(g, core, T, topo):
     V.wait_ge(S.vpmod, 1)
     V.tensor_scalar(T.pb[:], T.pmod[:], -4096.0, 2048.0 - 4096.0 * HI, Op.mult, Op.add).then_inc(S.vpb, 1)
     sels(8, 16)
-    V.tensor_scalar(T.nb[:], T.pmod[:], 4096.0, 4096.0 * HI - 2048.0, Op.mult, Op.add).then_inc(S.vnb, 1)
     V.memset(T.cst[:], 0.25).then_inc(S.vcst, 1)
+    V.tensor_scalar(T.nb[:], T.pmod[:], 4096.0, 4096.0 * HI - 2048.0, Op.mult, Op.add).then_inc(S.vnb, 1)
     V.memset(T.kva[:, 16:32], 0.0).then_inc(S.vkz, 1)
     V.memset(T.kvb[:, 16:32], 0.0).then_inc(S.vkz, 1)
+    V.tensor_scalar(T.half[:], T.d15[:, 0:16:8], 8.0, None, Op.is_lt).then_inc(S.vhalf, 1)
+    V.tensor_copy(T.parf[:, C0:C1], T.part[:, C0:C1]).then_inc(S.vidw, 1)
     V.wait_ge(S.vcst, 1)
     V.tensor_tensor_scan(T.c16r[:], T.cst[:], T.cst[:], -0.5, Op.add, Op.add).then_inc(S.vramp, 1)
     V.wait_ge(S.vtz, 1)
     V.tensor_scalar(T.tab[:, 15:143:16], T.ab[:, 0:128:16], 8.0, 4096.0, Op.is_lt, Op.mult).then_inc(S.vtab, 1)
     V.tensor_scalar(T.parlo[:], T.part[:], 127, None, Op.bitwise_and).then_inc(S.vpar, 1)
-    V.memset(T.cc[:, 0:32:2], 1.0).then_inc(S.vcc, 1)
-    V.memset(T.wv[:, NODE:NODE + 1], 0.0).then_inc(S.vzb, 1)
-    for k in (3, 2, 1, 0):
-        if "f%d" % k not in ORDER:
-            weight(k)
+    V.wait_ge(S.gdw, 1)
+    V.wait_ge(S.vhalf, 1)
+    for v in range(2):
+        V.tensor_scalar(T.idw[:, 144 * v:144 * v + 144], T.dw[:], 0.0, T.half[:, v:v + 1], Op.is_equal, Op.mult).then_inc(S.vidw, 1)
 
     def toks(b):
         P.wait_ge(S["vsel%d" % b], 4)
@@ -163,6 +180,11 @@ def rank_program(g, core, T, topo):
     def places(b):
         P.matmul(T["tr%d" % b][:, 0:512], T.grp[:], T.hx[:, 512 * b:512 * b + 512], b > 1, b < 2).then_inc(S["ptr%d" % b], 1)
 
+    def start(c):
+        c0, c1 = CH[c]
+        P.matmul(ps[c][:, 0:c1 - c0], T.cst[:], T.c16r[:, c0:c1], True, False).then_inc(S["pok%d" % c], 1)
+        P.matmul(ps[c][:, 0:c1 - c0], T.mr[0:4, :], T.cst[0:4, c0:c1], False, False).then_inc(S["pok%d" % c], 1)
+
     P.wait_ge(S.vtok, 1)
     toks(0)
     toks(1)
@@ -173,11 +195,16 @@ def rank_program(g, core, T, topo):
     for b in (2, 3):
         places(b)
         toks(b)
+    P.wait_ge(S.vidw, 3)
+    for v in range(2):
+        for t in range(2):
+            o = 144 * v + 8 - 8 * (t - v)
+            P.matmul(T.ps2[:, 64 + v:64 + K0:2], T.idw[:, o:o + 128], T.parf[:, C0 + t * K0 // 2:C0 + (t + 1) * K0 // 2],
+                     v + t == 0, v + t == 2).then_inc(S.ppar, 1)
     P.wait_ge(S.vramp, 1)
     P.wait_ge(S.gmr, 1)
-    for c, (c0, c1) in enumerate(CH):
-        P.matmul(ps[c][:, 0:c1 - c0], T.cst[:], T.c16r[:, c0:c1], True, False).then_inc(S["pok%d" % c], 1)
-        P.matmul(ps[c][:, 0:c1 - c0], T.mr[0:4, :], T.cst[0:4, c0:c1], False, False).then_inc(S["pok%d" % c], 1)
+    start(0)
+    start(1)
     P.wait_ge(S.vtab, 1)
 
     def zeros(k0, k1):
@@ -187,22 +214,18 @@ def rank_program(g, core, T, topo):
     A.wait_ge(S.gmb, 1)
     A.activation(T.ab[:], T.mb[:], Fn.Abs, bias=-7.5).then_inc(S.aab, 1)
     A.wait_ge(S.vz, 1)
-    zeros(0, ZR[0])
+    zeros(0, Z0)
+    A.wait_ge(S.ldown, 16)
+    A.activation(T.pm[:, 256:384], T.own[:], Fn.Copy).then_inc(S.aown, 1)
     A.wait_ge(S.vpb, 1)
-    nev = [0] * 4
-    for b in range(4):
-        cols = [x for x in range(32 * b, 32 * b + 32) if not any(meet((x, x + 1), m) for m in MS)]
-        for x in cols:
-            if x - 1 not in cols:
-                y = min(z for z in range(x, 32 * b + 33) if z not in cols)
-                A.wait_ge(S["ptr%d" % b], 5)
-                A.activation(tokx(16 * x, 16 * y), T["tr%d" % b][:, 16 * x - 512 * b:16 * y - 512 * b], Fn.Identity,
-                             bias=T.pb[:]).then_inc(S["ev%d" % b], 1)
-                nev[b] += 1
-        zeros(ZR[b], ZR[b + 1])
+    nb = MS[0][0] // 32
+    for b in range(nb):
+        A.wait_ge(S["ptr%d" % b], 5)
+        A.activation(tokx(512 * b, 512 * b + 512), T["tr%d" % b][:], Fn.Identity, bias=T.pb[:]).then_inc(S["ev%d" % b], 1)
+    zeros(Z0, Z1)
 
-    V.wait_ge(S.ldown, 16)
-    prev = T.own[:, 0:128]
+    V.wait_ge(S.aown, 1)
+    prev = T.pm[:, 256:384]
     for k in (1, 2):
         m = T.pm[:, 128 * k - 128:128 * k]
         V.wait_ge(S["arr%d" % k], ne[k])
@@ -211,59 +234,68 @@ def rank_program(g, core, T, topo):
             V.wait_ge(S.vpar, 1)
             V.tensor_copy(T.lo[:], T.parlo[:]).then_inc(S.vlist, 1)
         else:
-            V.tensor_scalar(T.pcol[:], T.part[:], NODE + 1.0, None, Op.add).then_inc(S.vpcol, 1)
+            V.tensor_scalar(T.pcol[:, C1:128], T.part[:, C1:128], NODE + 1.0, None, Op.add).then_inc(S.vpcol, 1)
         V.wait_ge(S["vm%d" % k], 1)
         prev = m
     V.wait_ge(S.arr3, ne[3])
     for h in range(2):
         V.tensor_tensor(T.mx[:, 64 * h:64 * h + 64], T.pm[:, 128 + 64 * h:192 + 64 * h], T.land3[:, 64 * h:64 * h + 64],
                         Op.max).then_inc(S["vm3%d" % h], 1)
+    tables(0)
     for h in range(2):
         V.wait_ge(S["vm3%d" % h], 1)
         V.tensor_scalar(T.tgt[:, 64 * h:64 * h + 64], T.mx[:, 64 * h:64 * h + 64], 4095, None, Op.bitwise_and).then_inc(S.vtgt, 1)
+    tables(1)
     for q in (V, A):
         q.wait_ge(S.vlist, 1)
         q.wait_ge(S.vtgt, 2)
     A.wait_ge(S.vnb, 1)
-    V.wait_ge(S.vpcol, 1)
 
-    neq = [sum(meet(m, ch) for m in MV + MS) for ch in CH]
+    UN = MV[:2] + CH[1:]
+    neq = [sum(meet(m, u) for m in MV + MS) for u in UN]
 
-    def piece(m):
-        return S["veq%d" % [meet(m, ch) for ch in CH].index(True)]
+    def unit(m):
+        return S["veq%d" % [meet(m, u) for u in UN].index(True)]
 
-    def rows_out(a, b):
-        for k in range(a // 32, (b + 31) // 32):
-            if nev[k]:
-                V.wait_ge(S["ev%d" % k], nev[k])
+    def got(a, b):
+        return tokx(16 * a, 16 * b) if a < LATE else T.gx[:, 16 * (a - LATE):16 * (b - LATE)]
 
     def match(k):
         a, b = MV[k]
-        rows_out(a, b)
+        for u in range(a // 32, (b + 31) // 32):
+            V.wait_ge(S["ev%d" % u], 1)
         V.tensor_tensor(T.eq[:, 16 * a:16 * b], T.tgt[:, 0:128].indirect(T.lo[:, a:b]), tokx(16 * a, 16 * b),
-                        Op.is_equal).then_inc(piece(MV[k]), 1)
+                        Op.is_equal).then_inc(unit(MV[k]), 1)
 
     def compare(k):
         a, b = MS[k]
-        u = a // 32
-        rows_out(a, b)
-        V.wait_ge(S["ptr%d" % u], 5)
+        V.wait_ge(S["ptr%d" % (a // 32)], 5)
         V.wait_ge(S["ag%d" % k], 1)
-        V.tensor_tensor(T.eq[:, 16 * a:16 * b], tokx(16 * a, 16 * b), T["tr%d" % u][:, 16 * a - 512 * u:16 * b - 512 * u],
-                        Op.is_equal).then_inc(piece(MS[k]), 1)
+        V.tensor_tensor(T.eq[:, 16 * a:16 * b], got(a, b), T["tr%d" % (a // 32)][:], Op.is_equal).then_inc(unit(MS[k]), 1)
 
     for k, (a, b) in enumerate(MS):
-        A.activation(tokx(16 * a, 16 * b), T.tgt[:, 0:128].indirect(T.lo[:, a:b]), Fn.Identity, bias=T.nb[:]).then_inc(
-            S["ag%d" % k], 1)
+        A.activation(got(a, b), T.tgt[:, 0:128].indirect(T.lo[:, a:b]), Fn.Identity, bias=T.nb[:]).then_inc(S["ag%d" % k], 1)
+        if k == 0:
+            A.wait_ge(S.ppar, 4)
+            A.activation(T.pcol[:, C0:C1], T.ps2[:, 64:64 + K0], Fn.Identity, bias=NODE + 1.0).then_inc(S.apc, 1)
     for c, (c0, c1) in enumerate(CH):
-        P.wait_ge(S["veq%d" % c], neq[c])
+        if c == 1:
+            P.wait_ge(S.apc, 1)
+            start(2)
         for i in range(16):
-            P.matmul(ps[c][:, 0:c1 - c0], T.tab[:, 15 - i:143 - i], T.eq[:, 16 * c0 + i:16 * c1:16],
-                     False, i == 15).then_inc(S["pok%d" % c], 1)
+            if c:
+                P.wait_ge(S["veq%d" % (c + 1)], neq[c + 1])
+                mov = T.eq[:, 16 * c0 + i:16 * c1:16]
+            else:
+                t, u = divmod(i, 8)
+                P.wait_ge(S["veq%d" % t], neq[t])
+                mov = T.eq[:, 16 * c0 + 8 * K0 * t + u:16 * c0 + 8 * K0 * (t + 1):8]
+            P.matmul(ps[c][:, 0:c1 - c0], T.tab[:, 15 - i:143 - i], mov, False, i == 15).then_inc(S["pok%d" % c], 1)
 
     def offsets(c):
         c0, c1 = CH[c]
         V.wait_ge(S["pok%d" % c], 18)
+        V.wait_ge(S.vpcol if c else S.apc, 1)
         V.tensor_tensor(T.off[:, c0:c1], ps[c][:, 0:c1 - c0], T.pcol[:, c0:c1], Op.min).then_inc(S["voff%d" % c], 1)
 
     def offsets_for(q, m):
@@ -277,105 +309,119 @@ def rank_program(g, core, T, topo):
             V.wait_ge(S.scv, k)
         else:
             V.wait_ge(S.vzb, 1)
-            V.wait_ge(S.gj0, 1)
-            for c in range(len(CH)):
-                V.wait_ge(S["veq%d" % c], neq[c])
+            V.wait_ge(S.glz, 1)
+            for c, u in enumerate(UN):
+                if u[0] < LATE:
+                    V.wait_ge(S["veq%d" % c], neq[c])
+        V.wait_ge(S["gj%d" % (k + 1)], 1)
         offsets_for(V, SV[k])
-        V.tensor_scalar(T.wv[:].indirect(T.off[:, a:b]), T.jrow[:, 0:16 * (b - a)], BIG, 16 * (a - SS[0][0]) * BIG,
+        V.tensor_scalar(T.wv[:].indirect(T.off[:, a:b]), T.jrow[:, 16 * a:16 * b], BIG, 16 * (a - SS[1][0]) * BIG * k,
                         Op.mult, Op.add).then_inc(S.scv, 1)
 
     for w in ORDER.split():
-        {"v": match, "c": compare, "o": offsets, "s": scatter, "f": weight}[w[0]](int(w[1]))
+        {"v": match, "c": compare, "o": offsets, "s": scatter, "f": tables}[w[0]](int(w[1]))
+    zeros(Z1, NZ)
     A.wait_ge(S.afa, NZ)
     for k, (a, b) in enumerate(SS):
-        A.wait_ge(S["gj%d" % k], 1)
+        A.wait_ge(S["gj%d" % (2 * k)], 1)
         offsets_for(A, SS[k])
         if k:
             A.wait_ge(S.sca, k)
-        A.activation(T.ww[:].indirect(T.off[:, a:b]), T.jrow[:, jr[k]:jr[k] + 16 * (b - a)], Fn.Silu).then_inc(S.sca, 1)
+        x = 16 * (C1 if k else a)
+        A.activation(T.ww[:].indirect(T.off[:, a:b]), T.jrow[:, x:x + 16 * (b - a)], Fn.Silu).then_inc(S.sca, 1)
 
-    def look(q, d, h):
+    def at(d):
+        return LS + 10 * (7 - d)
+
+    def one(d, c):
+        return at(d) + c - 5 * (c % 2)
+
+    def look(q, d, c):
         w = int(q is V)
-        win = (T.ww, T.wv)[w]
-        e0, b = 128 * d + 64 * h, LS + 28 - 4 * d + 2 * h
-        if d:
-            q.wait_ge(S["l%d%d" % (d - 1, h)], 2)
-            src, out = win[:, NODE:NODE + REG].indirect(T.ls[:, b:b + 2]), T.vs[:, e0 + w:e0 + 64:2]
-        elif h:
-            return
-        else:
-            src, out = win[:, NODE + 1:NODE + 65], T.vs[:, w:128:2]
+        q.wait_ge(S["l%d%d" % (d - 1, c)], 1)
+        src = (T.ww, T.wv)[w][:, NODE:NODE + REG].indirect(T.ls[:, one(d, c):one(d, c) + 1])
+        e0 = 33 * (4 * d + c - 4)
+        out = T.vs[:, e0 + w:e0 + 32:2]
         if w:
-            q.tensor_scalar(out, src, 1.0 / BIG, 0.25, Op.mult, Op.add).then_inc(S["y%d%d" % (d, h)], 1)
+            q.tensor_scalar(out, src, 1.0 / BIG, 0.25, Op.mult, Op.add).then_inc(S["y%d" % c], 1)
         else:
-            q.activation(out, src, Fn.Copy).then_inc(S["x%d%d" % (d, h)], 1)
+            q.activation(out, src, Fn.Copy).then_inc(S["x%d" % c], 1)
 
-    def scans(d, h):
+    def scan(d, c):
         for w in "yx":
-            V.wait_ge(S["%s%d%d" % (w, d, h if d else 0)], 1)
-        for c in (2 * h, 2 * h + 1):
-            b = 24 - 4 * d + c
-            V.tensor_tensor_scan(T.ls[:, b:b + LS + 1:4], T.vs[:, 128 * d + 32 * c:128 * d + 32 * c + 32], T.cc[:], 0.0,
-                                 Op.add, Op.mult).then_inc(S["l%d%d" % (d, h)], 1)
+            V.wait_ge(S["%s%d" % (w, c)], d)
+        b, e0 = at(d + 1) + c, 33 * (4 * d + c - 4)
+        V.tensor_tensor_scan(T.ls[:, b - 160:b + 1:5], T.vs[:, e0:e0 + 33], T.cc[:], 0.0, Op.add, Op.mult).then_inc(
+            S["l%d%d" % (d, c)], 1)
 
+    V.wait_ge(S.vcc, 7)
+    V.wait_ge(S.sca, len(SS))
+    for c in range(4):
+        V.tensor_tensor_scan(T.ra[:, 16 * c:16 * c + 16], T.ww[:, NODE + 1 + 16 * c:NODE + 17 + 16 * c], T.wa[:], 0.0,
+                             Op.add, Op.mult).then_inc(S["ra%d" % c], 1)
     V.wait_ge(S.scv, len(SV))
-    V.wait_ge(S.vcc, 3)
-    for d in range(7):
-        for step in (lambda h: look(V, d, h), lambda h: scans(d, h)):
-            step(0)
-            step(1)
+    for c in range(4):
+        V.wait_ge(S["ra%d" % c], 1)
+        V.tensor_tensor_scan(T.ls[:, one(1, c) - 75:one(1, c) + 1:5], T.wv[:, NODE + 1 + 16 * c:NODE + 17 + 16 * c], T.wb[:],
+                             T.ra[:, 16 * c + 15:16 * c + 16], Op.add, Op.mult).then_inc(S["l0%d" % c], 1)
+    for d in range(1, 7):
+        for c in range(4):
+            look(V, d, c)
+        if d == 1:
+            V.tensor_copy(T.ls[:, at(1) + 1:at(1) + 4:2], T.ls[:, one(1, 1):one(1, 3) + 1:2]).then_inc(S.lfix, 1)
+        for c in range(4):
+            scan(d, c)
 
     def list_of(q, d):
-        q.wait_ge(S["l%d0" % (d - 1)], 2)
-        q.wait_ge(S["l%d1" % (d - 1)], 2)
+        if d == 1:
+            q.wait_ge(S.lfix, 1)
+        for c in range(4):
+            q.wait_ge(S["l%d%d" % (d - 1, c)], 1)
 
     dst = cores[mate]
     rid, pid = topo.addr(dst, core)
     nl = len(topo.engines(core, dst))
-    m = 28 - 4 * EARLY
-    for d in range(1, EARLY + 1):
+    for d in range(1, 7):
         list_of(g, d)
-    g.remote_dma(T.k2[:, m:28], T.ls[:, LS + m:LS + 28], S.lst, S.lsent, pid, rid, topo.mask(core, dst))
-    for d in range(EARLY + 1, 8):
-        list_of(g, d)
-    g.remote_dma(T.k2[:, 0:m], T.ls[:, LS:LS + m], S.lst2, S.lsent, pid, rid, topo.mask(core, dst))
+    g.remote_dma(T.k2[:, at(6) - LS:at(1) + 4 - LS], T.ls[:, at(6):at(1) + 4], S.lst, S.lsent, pid, rid, topo.mask(core, dst))
+    list_of(g, 7)
+    g.remote_dma(T.k2[:, 0:4], T.ls[:, LS:LS + 4], S.lst2, S.lsent, pid, rid, topo.mask(core, dst))
     g.wait_ge(S.lsent, 2 * nl)
-    ka, kb = T.kva[:, 16:2065], T.kvb[:, 16:2065]
+
+    def keys(q, y, kv, d, lst, s0=0, s1=64):
+        out = T[y][:, 8 * s0 + d:8 * s1:8]
+        src = kv[:, 16:2065].indirect(lst) if d else kv[:, 17:81]
+        (q.tensor_copy(out, src) if q is V else q.activation(out, src, Fn.Copy)).then_inc(S[y], 1)
+
+    def own(q, d):
+        list_of(q, d)
+        keys(q, "ya", T.kva, d, T.ls[:, at(d):at(d) + 4])
+
     A.wait_ge(S.sca, len(SS))
-    for d in range(8):
-        if d < 7:
-            look(A, d, 0)
-            look(A, d, 1)
-        else:
-            list_of(A, d)
-        if d == 0:
-            A.wait_ge(S.ldkv, 16)
-        src = ka.indirect(T.ls[:, LS + 28 - 4 * d:LS + 32 - 4 * d]) if d else T.kva[:, 17:81]
-        A.activation(T.ya[:, d:512:8], src, Fn.Copy).then_inc(S.aya, 1)
-    Y.wait_ge(S.aya, 8)
+    A.wait_ge(S.ldkv, 16)
+    V.wait_ge(S.ldkv, 16)
+    keys(A, "ya", T.kva, 0, None)
+    for d in range(1, 7):
+        for c in range(4):
+            look(A, d, c)
+        if d in KIN:
+            own(A, d)
+    for d in range(1, 8):
+        if d not in KIN:
+            own(V if d in KVO else A, d)
+    Y.wait_ge(S.ya, 8)
     Y.wait_ge(S.lsent, 2 * nl)
     Y.dma_start(T.y[:, 512 * mine:512 * mine + 512], T.ya[:]).then_inc(S.st1, 16)
-    V.wait_ge(S.ldkw, 16)
-    A.wait_ge(S.ldkw, 16)
-    V.tensor_copy(T.yb[:, 0:512:8], T.kvb[:, 17:81]).then_inc(S.vyb, 1)
-
-    def keys(d, v):
-        out, src = T.yb[:, d:512:8], kb.indirect(T.k2[:, 28 - 4 * d:32 - 4 * d])
-        if v:
-            V.tensor_copy(out, src).then_inc(S.vyb, 1)
-        else:
-            A.activation(out, src, Fn.Copy).then_inc(S.ayb, 1)
-
-    V.wait_ge(S.lst, nl)
-    A.wait_ge(S.lst, nl)
-    for d in range(1, EARLY + 1):
-        keys(d, d in KV1)
-    V.wait_ge(S.lst2, nl)
-    A.wait_ge(S.lst2, nl)
-    for d in range(EARLY + 1, 8):
-        keys(d, d in KV2)
-    nk = 1 + len(KV1) + len(KV2)
-    Y.wait_ge(S.vyb, nk)
-    Y.wait_ge(S.ayb, 8 - nk)
+    for q in (V, A):
+        q.wait_ge(S.ldkw, 16)
+    keys(V, "yb", T.kvb, 0, None)
+    for q in (V, A):
+        q.wait_ge(S.lst, nl)
+    for d in range(1, 7):
+        keys(V if d in KV1 else A, "yb", T.kvb, d, T.k2[:, at(d) - LS:at(d) - LS + 4])
+    for h, q in enumerate((V, A)):
+        q.wait_ge(S.lst2, nl)
+        keys(q, "yb", T.kvb, 7, T.k2[:, 2 * h:2 * h + 2], 32 * h, 32 * h + 32)
+    Y.wait_ge(S.yb, 9)
     Y.dma_start(T.y[:, 512 * other:512 * other + 512], T.yb[:]).then_inc(S.st1, 16)
     Y.wait_ge(S.st1, 32)

from concourse.mybir import AluOpType as Op, ActivationFunctionType as Fn

CH = [(4, 48), (48, 96), (96, 128)]
MV = [(4, 26), (26, 48), (48, 64)]
MS = [(64, 96), (96, 128)]
LATE = 96
SS = [(4, 34), (94, 128)]
SV = [(34, 48), (48, 94)]
ORDER = "v0 v1 v2 c0 o0 c1 s0 o1 f2 o2 s1"
NODE, REG = 2048, 2049
BIG = 2.0 ** 30
ZC = 257
NZ = 8
Z0, Z1 = 4, 8
LS = 160
HI = 144.0
SP = {1: slice(0, None, 2), 2: slice(1, None, 2), 3: slice(0, None)}
W = 2.0 ** 24
KIN, KVO = (2, 4, 6), (1, 3)
KV1 = (1, 2, 3)

I32 = ("sbuf", [128, 128], "int32")
U16 = ("sbuf", [128, 128], "uint16")
B16 = ("sbuf", [128, 128], "bfloat16")
F16 = ("sbuf", [128, 128], "float16")
PS = ("psum", [128, 512], "float32")


def sb(k, d="float32"):
    return ("sbuf", [128, k], d)


SCRATCH = {
    "own": I32, "snd": ("dram", [3, 128, 128], "int32"), "land1": I32, "land2": I32, "land3": I32, "mx": I32, "tgt": I32,
    "tokc": I32, "tokf": F16, "part": I32, "parlo": I32, "parf": F16, "lo": U16, "hif": B16, "pcol": sb(128),
    "sm": sb(16, "int32"), "d15": sb(16, "int32"), "pmod": sb(1), "pb": sb(1), "nb": sb(1), "mb": B16, "ab": B16,
    "grp": B16, "mcol": sb(16, "bfloat16"), "hx": sb(2048, "bfloat16"), "half": sb(2), "dw": sb(144, "bfloat16"),
    "idw": sb(288, "float16"), "sel": sb(2048, "float16"), "tab": sb(144, "float16"), "cst": B16, "mr": B16, "c16r": B16,
    "cc": sb(33), "c1": sb(16), "c2": sb(16), "wa": sb(16), "wb": sb(16), "ra": sb(64), "jrow": sb(2048),
    "eq": sb(2048, "float16"), "off": U16, "gx": sb(16 * (128 - LATE)), "zero": sb(ZC), "ww": sb(NODE + NZ * ZC),
    "wv": sb(NODE + REG), "vs": sb(792), "ls": sb(LS + 64, "uint16"), "k2": sb(64, "uint16"),
    "kva": sb(2080, "bfloat16"), "kvb": sb(2080, "bfloat16"), "ya": sb(512, "bfloat16"), "yb": sb(512, "bfloat16"),
    "tr0": PS, "tr1": PS, "tr2": PS, "tr3": PS, "ps0": PS, "ps1": PS, "ps2": PS, "pm": PS,
}
SEMAPHORES = (["ld1", "ld2", "ld3", "ldown", "ldtok", "ldpar", "ldkv", "ldkw", "sent", "arr1", "arr2", "arr3", "lst", "lst2",
               "lsent", "st1", "gmr", "gsm", "gmb", "gdw", "gj0", "gj1", "gj2", "vramp", "vtz", "vc1", "vc3", "vcc", "vz", "vzb",
               "vkz", "vcst", "vtok", "vpar", "vpcol", "vhf", "vhx", "vlist", "vpmod", "vpb", "vnb", "vtab", "vd15", "vmcol",
               "vhalf", "vidw", "vgrp", "vm1", "vm2", "vm30", "vm31", "vtgt", "aab", "aown", "glz", "apc", "afa", "ppar",
               "sca", "scv", "lfix", "ya", "yb"]
              + ["%s%d" % (w, c) for w in ("vsel", "ev", "ptr", "veq", "ra", "x", "y") for c in range(4)]
              + ["%s%d" % (w, c) for w in ("pok", "voff") for c in range(len(CH))] + ["ag%d" % k for k in range(len(MS))]
              + ["l%d%d" % (d, c) for d in range(7) for c in range(4)])


def meet(a, b):
    return a[0] < b[1] and b[0] < a[1]


def rank_program(g, core, T, topo):
    r = T.rank_of(core)
    if r is None:
        return
    S = T.sem
    cores = T.cores
    n = len(cores)
    V, A, P, Y = g.vector, g.scalar, g.tensor, g.sync
    mate = (r + 2) % n
    mine, other = r // 2, 1 - r // 2
    low = {"allow_small_or_imprecise_dtypes": True}
    ps = [T.ps0, T.ps1, T.ps2]
    C0, C1 = CH[0]
    K0 = C1 - C0

    def blk(q):
        return T.best[:, q * 2048:(q + 1) * 2048]

    def tokx(a, b):
        return T.wv[:, NODE + 1 + a:NODE + 1 + b]

    Y.dma_start(T.snd[0], blk((r + 1) % n)).then_inc(S.ld1, 16)
    Y.dma_start(T.part[:], T.par[:]).then_inc(S.ldpar, 16)
    Y.dma_start(T.tokc[:], T.tok[:]).then_inc(S.ldtok, 16)
    Y.dma_start(T.snd[1], blk((r + 2) % n)).then_inc(S.ld2, 16)
    Y.dma_start(T.snd[2], blk((r + 3) % n)).then_inc(S.ld3, 16)
    Y.dma_start(T.own[:], blk(r)).then_inc(S.ldown, 16)
    eng = {k: topo.engines(core, cores[(r + k) % n])[SP[k]] for k in (1, 2, 3)}
    ne = {k: len(eng[k]) for k in eng}
    Y.wait_ge(S.vkz, 2)
    Y.wait_ge(S.sent, sum(ne.values()))
    Y.dma_start(T.kva[:, 17:2065], T.kv[:, mine * 2048:(mine + 1) * 2048]).then_inc(S.ldkv, 16)
    Y.dma_start(T.kvb[:, 17:2065], T.kv[:, other * 2048:(other + 1) * 2048]).then_inc(S.ldkw, 16)

    g.iota(T.mb[:], [[-16, 8], [0, 16]], 0, 1, **low).then_inc(S.gmb, 1)
    g.iota(T.sm[:], [[-1, 16]], 0, 1).then_inc(S.gsm, 1)
    for k in (1, 2, 3):
        rid, pid = topo.addr(cores[(r + k) % n], core)
        g.wait_ge(S["ld%d" % k], 16)
        g.remote_dma(T["land%d" % k][:], T.snd[k - 1], S["arr%d" % k], S.sent, pid, rid, sum(1 << e for e in eng[k]))
    g.iota(T.dw[:], [[1, 144]], -8, -1, **low).then_inc(S.gdw, 1)
    g.iota(T.mr[0:32, :], [[0, 8], [1, 16]], 0, 0, **low).then_inc(S.gmr, 1)
    for k, (a, b) in enumerate((SS[0], SV[0])):
        g.iota(T.jrow[:, 16 * a:16 * b], [[8, b - a], [8 * K0, 2], [1, 8]], 16 * C0 + 8 * (a - C0) + 1, 0, **low).then_inc(
            S["gj%d" % k], 1)
    g.iota(tokx(16 * LATE, 2048), [[0, 2048 - 16 * LATE]], 0, 0, **low).then_inc(S.glz, 1)
    nj = 16 * max(b - a for a, b in (SS[1], SV[1]))
    g.iota(T.jrow[:, 16 * C1:16 * C1 + nj], [[1, nj]], 16 * SS[1][0] + 1, 0, **low).then_inc(S.gj2, 1)

    def sels(a0, a1):
        for a in range(a0, a1):
            V.tensor_scalar(T.sel[:, 128 * a:128 * a + 128], T.mb[:], float(a), None, Op.is_equal).then_inc(S["vsel%d" % (a // 4)], 1)

    def tables(k):
        if k == 0:
            V.tensor_scalar(T.c1[:], T.d15[:], 0.0, W, Op.is_equal, Op.mult).then_inc(S.vc1, 1)
            V.tensor_scalar(T.c2[:], T.d15[:], 1.0, None, Op.not_equal).then_inc(S.vc1, 1)
        elif k == 1:
            V.tensor_scalar(T.cc[:, 31:32], T.pmod[:], 15.0, 1.0 / W, Op.is_equal, Op.max).then_inc(S.vc3, 1)
            V.wait_ge(S.vc1, 2)
            V.tensor_tensor(T.wa[:], T.c1[:], T.c2[:], Op.max).then_inc(S.vc3, 1)
            V.tensor_tensor(T.cc[:, 1:31:2], T.c1[:, 0:15], T.c2[:, 0:15], Op.max).then_inc(S.vcc, 1)
        elif k == 2:
            V.wait_ge(S.vc3, 2)
            V.tensor_scalar(T.wb[:, 0:15], T.wa[:, 0:15], 1.0 / W, None, Op.max).then_inc(S.vcc, 1)
            V.tensor_scalar(T.wa[:, 15:16], T.wa[:, 15:16], 1.0 / W, BIG, Op.max, Op.mult).then_inc(S.vcc, 1)
            A.wait_ge(S.vc3, 2)
            A.activation(T.wb[:, 15:16], T.cc[:, 31:32], Fn.Copy, scale=(1 + 2.0 ** -13) / BIG).then_inc(S.vcc, 1)
        else:
            V.memset(T.wv[:, NODE:NODE + 1], 0.0).then_inc(S.vzb, 1)
            V.memset(T.cc[:, 0:33:2], 1.0).then_inc(S.vcc, 1)
            V.memset(T.vs[:, 32:792:33], 0.0).then_inc(S.vcc, 1)
            V.memset(T.ls[:, LS:LS + 64], 0).then_inc(S.vcc, 1)

    V.memset(T.zero[:], 0.0).then_inc(S.vz, 1)
    V.memset(T.tab[:], 0.0).then_inc(S.vtz, 1)
    tables(3)
    V.wait_ge(S.gmb, 1)
    sels(0, 4)
    V.wait_ge(S.gsm, 1)
    V.tensor_scalar(T.d15[:], T.sm[:], 15, None, Op.bitwise_and).then_inc(S.vd15, 1)
    sels(4, 8)
    V.wait_ge(S.vd15, 1)
    V.tensor_scalar(T.mcol[:], T.d15[:], 0.0, None, Op.is_equal).then_inc(S.vmcol, 1)
    V.tensor_copy(T.pmod[:], T.d15[:, 0:1]).then_inc(S.vpmod, 1)
    V.wait_ge(S.aab, 1)
    V.tensor_scalar(T.grp[:], T.ab[:], 8.0, 4096.0, Op.is_lt, Op.mult).then_inc(S.vgrp, 1)
    V.wait_ge(S.ldpar, 16)
    V.tensor_scalar(T.hif[:], T.part[:], 1.0 / 128, HI - 63.5 / 128, Op.mult, Op.add).then_inc(S.vhf, 1)
    V.wait_ge(S.ldtok, 16)
    V.tensor_scalar(T.tokf[:], T.tokc[:], -2048.0, None, Op.add).then_inc(S.vtok, 1)
    V.wait_ge(S.vmcol, 1)
    V.wait_ge(S.vhf, 1)
    for i in range(16):
        V.tensor_scalar(T.hx[:, i:2048:16], T.hif[:], T.mcol[:, i:i + 1], None, Op.mult).then_inc(S.vhx, 1)
    V.wait_ge(S.vpmod, 1)
    V.tensor_scalar(T.pb[:], T.pmod[:], -4096.0, 2048.0 - 4096.0 * HI, Op.mult, Op.add).then_inc(S.vpb, 1)
    sels(8, 16)
    V.memset(T.cst[:], 0.25).then_inc(S.vcst, 1)
    V.tensor_scalar(T.nb[:], T.pmod[:], 4096.0, 4096.0 * HI - 2048.0, Op.mult, Op.add).then_inc(S.vnb, 1)
    V.memset(T.kva[:, 16:32], 0.0).then_inc(S.vkz, 1)
    V.memset(T.kvb[:, 16:32], 0.0).then_inc(S.vkz, 1)
    V.tensor_scalar(T.half[:], T.d15[:, 0:16:8], 8.0, None, Op.is_lt).then_inc(S.vhalf, 1)
    V.tensor_copy(T.parf[:, C0:C1], T.part[:, C0:C1]).then_inc(S.vidw, 1)
    V.wait_ge(S.vcst, 1)
    V.tensor_tensor_scan(T.c16r[:], T.cst[:], T.cst[:], -0.5, Op.add, Op.add).then_inc(S.vramp, 1)
    V.wait_ge(S.vtz, 1)
    V.tensor_scalar(T.tab[:, 15:143:16], T.ab[:, 0:128:16], 8.0, 4096.0, Op.is_lt, Op.mult).then_inc(S.vtab, 1)
    V.tensor_scalar(T.parlo[:], T.part[:], 127, None, Op.bitwise_and).then_inc(S.vpar, 1)
    V.wait_ge(S.gdw, 1)
    V.wait_ge(S.vhalf, 1)
    for v in range(2):
        V.tensor_scalar(T.idw[:, 144 * v:144 * v + 144], T.dw[:], 0.0, T.half[:, v:v + 1], Op.is_equal, Op.mult).then_inc(S.vidw, 1)

    def toks(b):
        P.wait_ge(S["vsel%d" % b], 4)
        for k in range(4):
            a = 4 * b + k
            P.matmul(T["tr%d" % b][:, 128 * k:128 * k + 128], T.sel[:, 128 * a:128 * a + 128], T.tokf[:], b < 2 and k == 0,
                     b > 1 and k == 3).then_inc(S["ptr%d" % b], 1)

    def places(b):
        P.matmul(T["tr%d" % b][:, 0:512], T.grp[:], T.hx[:, 512 * b:512 * b + 512], b > 1, b < 2).then_inc(S["ptr%d" % b], 1)

    def start(c):
        c0, c1 = CH[c]
        P.matmul(ps[c][:, 0:c1 - c0], T.cst[:], T.c16r[:, c0:c1], True, False).then_inc(S["pok%d" % c], 1)
        P.matmul(ps[c][:, 0:c1 - c0], T.mr[0:4, :], T.cst[0:4, c0:c1], False, False).then_inc(S["pok%d" % c], 1)

    P.wait_ge(S.vtok, 1)
    toks(0)
    toks(1)
    P.wait_ge(S.vgrp, 1)
    P.wait_ge(S.vhx, 16)
    places(0)
    places(1)
    for b in (2, 3):
        places(b)
        toks(b)
    P.wait_ge(S.vidw, 3)
    for v in range(2):
        for t in range(2):
            o = 144 * v + 8 - 8 * (t - v)
            P.matmul(T.ps2[:, 64 + v:64 + K0:2], T.idw[:, o:o + 128], T.parf[:, C0 + t * K0 // 2:C0 + (t + 1) * K0 // 2],
                     v + t == 0, v + t == 2).then_inc(S.ppar, 1)
    P.wait_ge(S.vramp, 1)
    P.wait_ge(S.gmr, 1)
    start(0)
    start(1)
    P.wait_ge(S.vtab, 1)

    def zeros(k0, k1):
        for k in range(k0, k1):
            A.activation(T.ww[:, NODE + ZC * k:NODE + ZC * k + ZC], T.zero[:], Fn.Silu).then_inc(S.afa, 1)

    A.wait_ge(S.gmb, 1)
    A.activation(T.ab[:], T.mb[:], Fn.Abs, bias=-7.5).then_inc(S.aab, 1)
    A.wait_ge(S.vz, 1)
    zeros(0, Z0)
    A.wait_ge(S.ldown, 16)
    A.activation(T.pm[:, 256:384], T.own[:], Fn.Copy).then_inc(S.aown, 1)
    A.wait_ge(S.vpb, 1)
    nb = MS[0][0] // 32
    for b in range(nb):
        A.wait_ge(S["ptr%d" % b], 5)
        A.activation(tokx(512 * b, 512 * b + 512), T["tr%d" % b][:], Fn.Identity, bias=T.pb[:]).then_inc(S["ev%d" % b], 1)
    zeros(Z0, Z1)

    V.wait_ge(S.aown, 1)
    prev = T.pm[:, 256:384]
    for k in (1, 2):
        m = T.pm[:, 128 * k - 128:128 * k]
        V.wait_ge(S["arr%d" % k], ne[k])
        V.tensor_tensor(m, prev, T["land%d" % k][:], Op.max).then_inc(S["vm%d" % k], 1)
        if k == 1:
            V.wait_ge(S.vpar, 1)
            V.tensor_copy(T.lo[:], T.parlo[:]).then_inc(S.vlist, 1)
        else:
            V.tensor_scalar(T.pcol[:, C1:128], T.part[:, C1:128], NODE + 1.0, None, Op.add).then_inc(S.vpcol, 1)
        V.wait_ge(S["vm%d" % k], 1)
        prev = m
    V.wait_ge(S.arr3, ne[3])
    for h in range(2):
        V.tensor_tensor(T.mx[:, 64 * h:64 * h + 64], T.pm[:, 128 + 64 * h:192 + 64 * h], T.land3[:, 64 * h:64 * h + 64],
                        Op.max).then_inc(S["vm3%d" % h], 1)
    tables(0)
    for h in range(2):
        V.wait_ge(S["vm3%d" % h], 1)
        V.tensor_scalar(T.tgt[:, 64 * h:64 * h + 64], T.mx[:, 64 * h:64 * h + 64], 4095, None, Op.bitwise_and).then_inc(S.vtgt, 1)
    tables(1)
    for q in (V, A):
        q.wait_ge(S.vlist, 1)
        q.wait_ge(S.vtgt, 2)
    A.wait_ge(S.vnb, 1)

    UN = MV[:2] + CH[1:]
    neq = [sum(meet(m, u) for m in MV + MS) for u in UN]

    def unit(m):
        return S["veq%d" % [meet(m, u) for u in UN].index(True)]

    def got(a, b):
        return tokx(16 * a, 16 * b) if a < LATE else T.gx[:, 16 * (a - LATE):16 * (b - LATE)]

    def match(k):
        a, b = MV[k]
        for u in range(a // 32, (b + 31) // 32):
            V.wait_ge(S["ev%d" % u], 1)
        V.tensor_tensor(T.eq[:, 16 * a:16 * b], T.tgt[:, 0:128].indirect(T.lo[:, a:b]), tokx(16 * a, 16 * b),
                        Op.is_equal).then_inc(unit(MV[k]), 1)

    def compare(k):
        a, b = MS[k]
        V.wait_ge(S["ptr%d" % (a // 32)], 5)
        V.wait_ge(S["ag%d" % k], 1)
        V.tensor_tensor(T.eq[:, 16 * a:16 * b], got(a, b), T["tr%d" % (a // 32)][:], Op.is_equal).then_inc(unit(MS[k]), 1)

    for k, (a, b) in enumerate(MS):
        A.activation(got(a, b), T.tgt[:, 0:128].indirect(T.lo[:, a:b]), Fn.Identity, bias=T.nb[:]).then_inc(S["ag%d" % k], 1)
        if k == 0:
            A.wait_ge(S.ppar, 4)
            A.activation(T.pcol[:, C0:C1], T.ps2[:, 64:64 + K0], Fn.Identity, bias=NODE + 1.0).then_inc(S.apc, 1)
    for c, (c0, c1) in enumerate(CH):
        if c == 1:
            P.wait_ge(S.apc, 1)
            start(2)
        for i in range(16):
            if c:
                P.wait_ge(S["veq%d" % (c + 1)], neq[c + 1])
                mov = T.eq[:, 16 * c0 + i:16 * c1:16]
            else:
                t, u = divmod(i, 8)
                P.wait_ge(S["veq%d" % t], neq[t])
                mov = T.eq[:, 16 * c0 + 8 * K0 * t + u:16 * c0 + 8 * K0 * (t + 1):8]
            P.matmul(ps[c][:, 0:c1 - c0], T.tab[:, 15 - i:143 - i], mov, False, i == 15).then_inc(S["pok%d" % c], 1)

    def offsets(c):
        c0, c1 = CH[c]
        V.wait_ge(S["pok%d" % c], 18)
        V.wait_ge(S.vpcol if c else S.apc, 1)
        V.tensor_tensor(T.off[:, c0:c1], ps[c][:, 0:c1 - c0], T.pcol[:, c0:c1], Op.min).then_inc(S["voff%d" % c], 1)

    def offsets_for(q, m):
        for c, ch in enumerate(CH):
            if meet(m, ch):
                q.wait_ge(S["voff%d" % c], 1)

    def scatter(k):
        a, b = SV[k]
        if k:
            V.wait_ge(S.scv, k)
        else:
            V.wait_ge(S.vzb, 1)
            V.wait_ge(S.glz, 1)
            for c, u in enumerate(UN):
                if u[0] < LATE:
                    V.wait_ge(S["veq%d" % c], neq[c])
        V.wait_ge(S["gj%d" % (k + 1)], 1)
        offsets_for(V, SV[k])
        V.tensor_scalar(T.wv[:].indirect(T.off[:, a:b]), T.jrow[:, 16 * a:16 * b], BIG, 16 * (a - SS[1][0]) * BIG * k,
                        Op.mult, Op.add).then_inc(S.scv, 1)

    for w in ORDER.split():
        {"v": match, "c": compare, "o": offsets, "s": scatter, "f": tables}[w[0]](int(w[1]))
    zeros(Z1, NZ)
    A.wait_ge(S.afa, NZ)
    for k, (a, b) in enumerate(SS):
        A.wait_ge(S["gj%d" % (2 * k)], 1)
        offsets_for(A, SS[k])
        if k:
            A.wait_ge(S.sca, k)
        x = 16 * (C1 if k else a)
        A.activation(T.ww[:].indirect(T.off[:, a:b]), T.jrow[:, x:x + 16 * (b - a)], Fn.Silu).then_inc(S.sca, 1)

    def at(d):
        return LS + 10 * (7 - d)

    def one(d, c):
        return at(d) + c - 5 * (c % 2)

    def look(q, d, c):
        w = int(q is V)
        q.wait_ge(S["l%d%d" % (d - 1, c)], 1)
        src = (T.ww, T.wv)[w][:, NODE:NODE + REG].indirect(T.ls[:, one(d, c):one(d, c) + 1])
        e0 = 33 * (4 * d + c - 4)
        out = T.vs[:, e0 + w:e0 + 32:2]
        if w:
            q.tensor_scalar(out, src, 1.0 / BIG, 0.25, Op.mult, Op.add).then_inc(S["y%d" % c], 1)
        else:
            q.activation(out, src, Fn.Copy).then_inc(S["x%d" % c], 1)

    def scan(d, c):
        for w in "yx":
            V.wait_ge(S["%s%d" % (w, c)], d)
        b, e0 = at(d + 1) + c, 33 * (4 * d + c - 4)
        V.tensor_tensor_scan(T.ls[:, b - 160:b + 1:5], T.vs[:, e0:e0 + 33], T.cc[:], 0.0, Op.add, Op.mult).then_inc(
            S["l%d%d" % (d, c)], 1)

    V.wait_ge(S.vcc, 7)
    V.wait_ge(S.sca, len(SS))
    for c in range(4):
        V.tensor_tensor_scan(T.ra[:, 16 * c:16 * c + 16], T.ww[:, NODE + 1 + 16 * c:NODE + 17 + 16 * c], T.wa[:], 0.0,
                             Op.add, Op.mult).then_inc(S["ra%d" % c], 1)
    V.wait_ge(S.scv, len(SV))
    for c in range(4):
        V.wait_ge(S["ra%d" % c], 1)
        V.tensor_tensor_scan(T.ls[:, one(1, c) - 75:one(1, c) + 1:5], T.wv[:, NODE + 1 + 16 * c:NODE + 17 + 16 * c], T.wb[:],
                             T.ra[:, 16 * c + 15:16 * c + 16], Op.add, Op.mult).then_inc(S["l0%d" % c], 1)
    for d in range(1, 7):
        for c in range(4):
            look(V, d, c)
        if d == 1:
            V.tensor_copy(T.ls[:, at(1) + 1:at(1) + 4:2], T.ls[:, one(1, 1):one(1, 3) + 1:2]).then_inc(S.lfix, 1)
        for c in range(4):
            scan(d, c)

    def list_of(q, d):
        if d == 1:
            q.wait_ge(S.lfix, 1)
        for c in range(4):
            q.wait_ge(S["l%d%d" % (d - 1, c)], 1)

    dst = cores[mate]
    rid, pid = topo.addr(dst, core)
    nl = len(topo.engines(core, dst))
    for d in range(1, 7):
        list_of(g, d)
    g.remote_dma(T.k2[:, at(6) - LS:at(1) + 4 - LS], T.ls[:, at(6):at(1) + 4], S.lst, S.lsent, pid, rid, topo.mask(core, dst))
    list_of(g, 7)
    g.remote_dma(T.k2[:, 0:4], T.ls[:, LS:LS + 4], S.lst2, S.lsent, pid, rid, topo.mask(core, dst))
    g.wait_ge(S.lsent, 2 * nl)

    def keys(q, y, kv, d, lst, s0=0, s1=64):
        out = T[y][:, 8 * s0 + d:8 * s1:8]
        src = kv[:, 16:2065].indirect(lst) if d else kv[:, 17:81]
        (q.tensor_copy(out, src) if q is V else q.activation(out, src, Fn.Copy)).then_inc(S[y], 1)

    def own(q, d):
        list_of(q, d)
        keys(q, "ya", T.kva, d, T.ls[:, at(d):at(d) + 4])

    A.wait_ge(S.sca, len(SS))
    A.wait_ge(S.ldkv, 16)
    V.wait_ge(S.ldkv, 16)
    keys(A, "ya", T.kva, 0, None)
    for d in range(1, 7):
        for c in range(4):
            look(A, d, c)
        if d in KIN:
            own(A, d)
    for d in range(1, 8):
        if d not in KIN:
            own(V if d in KVO else A, d)
    Y.wait_ge(S.ya, 8)
    Y.wait_ge(S.lsent, 2 * nl)
    Y.dma_start(T.y[:, 512 * mine:512 * mine + 512], T.ya[:]).then_inc(S.st1, 16)
    for q in (V, A):
        q.wait_ge(S.ldkw, 16)
    keys(V, "yb", T.kvb, 0, None)
    for q in (V, A):
        q.wait_ge(S.lst, nl)
    for d in range(1, 7):
        keys(V if d in KV1 else A, "yb", T.kvb, d, T.k2[:, at(d) - LS:at(d) - LS + 4])
    for h, q in enumerate((V, A)):
        q.wait_ge(S.lst2, nl)
        keys(q, "yb", T.kvb, 7, T.k2[:, 2 * h:2 * h + 2], 32 * h, 32 * h + 32)
    Y.wait_ge(S.yb, 9)
    Y.dma_start(T.y[:, 512 * other:512 * other + 512], T.yb[:]).then_inc(S.st1, 16)
    Y.wait_ge(S.st1, 32)
